import numpy as np
import ml_dtypes


def mxq(x, axis, fmt="e4m3"):
    dtype, down = {"e4m3": (ml_dtypes.float8_e4m3fn, 7), "e5m2": (ml_dtypes.float8_e5m2, 14)}[fmt]
    v = np.moveaxis(np.asarray(x, np.float32).astype(ml_dtypes.bfloat16).astype(np.float64), axis, -1)
    blocks = v.reshape(v.shape[:-1] + (-1, 32))
    amax = np.abs(blocks).max(-1, keepdims=True)
    byte = np.maximum(np.where(amax > 0, np.frexp(amax)[1] - 1 + 127, 0) - down, 1)
    scale = np.exp2(byte - 127.0)
    codes = (blocks / scale).astype(np.float32).astype(dtype).astype(np.float64)
    return np.moveaxis((codes * scale).reshape(v.shape), -1, axis)


WIDE = False


def mx_kscale(k):
    if not WIDE:
        return np.ones(k)
    levels = np.array([10, -10, 5, -5, 0])
    if k % 512:
        return np.exp2(np.random.permutation(np.resize(levels, k // 32))).repeat(32)
    a = np.empty((k // 512, 16))
    for p in range(k // 512):
        a[p, :8] = np.random.permutation(np.resize(levels, 8))
        for g in range(8):
            far = levels[np.abs(levels - a[p, g]) >= 10]
            a[p, g + 8] = far[np.random.randint(len(far))]
    return np.exp2(a.ravel()).repeat(32)


def f64(x):
    return np.asarray(x).astype(np.float64)


def striped(idx):
    return np.tile(idx.reshape(-1, 16).T, (8, 1)).astype(np.uint16)


def unstriped(offs):
    return offs[:16].T.reshape(-1).astype(np.int64)


def pack_weight(w):
    k, n = w.shape
    w = f64(np.asarray(w, np.float32).astype(ml_dtypes.bfloat16)).reshape(k // 32, 32, n)
    amax = np.abs(w).max(1)
    byte = np.clip(np.where(amax > 0, np.frexp(amax)[1] - 1 + 127 - 7, 1), 1, 254)
    scaled = (w * np.exp2(127.0 - byte)[:, None, :]).reshape(k, n).astype(np.float32)
    words = np.ascontiguousarray(scaled.reshape(k // 512, 128, 4, n).transpose(0, 1, 3, 2)).astype(ml_dtypes.float8_e4m3fn).view(np.uint8)
    return words, np.ascontiguousarray(byte.astype(np.uint8).reshape(k // 512, 16, n))


def unpack_weight(words, scales):
    g, p, n, _ = words.shape
    vals = np.ascontiguousarray(words).view(ml_dtypes.float8_e4m3fn).astype(np.float64) * np.repeat(np.exp2(scales.astype(np.float64) - 127.0), 8, axis=1)[..., None]
    return vals.transpose(0, 1, 3, 2).reshape(g * 512, n)


E2M1 = np.array([0.0, 0.5, 1.0, 1.5, 2.0, 3.0, 4.0, 6.0, -0.0, -0.5, -1.0, -1.5, -2.0, -3.0, -4.0, -6.0])


def pack_fp4(w):
    k, n = w.shape
    w = f64(np.asarray(w, np.float32).astype(ml_dtypes.bfloat16)).reshape(k // 32, 32, n)
    amax = np.abs(w).max(1)
    mant, ex = np.frexp(amax / 6.0)
    byte = np.clip(np.where(amax > 0, np.where(mant > 0.5, ex, ex - 1) + 127, 1), 1, 254)
    scaled = (w * np.exp2(127.0 - byte)[:, None, :]).reshape(k, n).astype(np.float32)
    c = np.ascontiguousarray(scaled.reshape(k // 512, 128, 4, n).transpose(0, 1, 3, 2)).astype(ml_dtypes.float4_e2m1fn).view(np.uint8) & 0xF
    words = (c[..., 0::2] | (c[..., 1::2] << 4)).reshape(k // 512, 128, 2 * n)
    return np.ascontiguousarray(words), np.ascontiguousarray(byte.astype(np.uint8).reshape(k // 512, 16, n))


def unpack_fp4(words, scales):
    g, _, n = scales.shape
    words = np.ascontiguousarray(words).reshape(g, 128, n, 2)
    nib = np.empty((g, 128, n, 4), np.uint8)
    nib[..., 0::2] = words & 0xF
    nib[..., 1::2] = words >> 4
    vals = E2M1[nib] * np.repeat(np.exp2(scales.astype(np.float64) - 127.0), 8, axis=1)[..., None]
    return vals.transpose(0, 1, 3, 2).reshape(g * 512, n)


def planes(y):
    n, m = y.shape
    v = y.astype(np.float32).astype(ml_dtypes.bfloat16).astype(np.float64).reshape(n // 32, 32, m)
    top = np.abs(v).max(1)
    byte = np.clip(np.where(top > 0, np.frexp(top)[1] - 1 + 127 - 7, 1), 1, 254)
    codes = (v * np.exp2(127.0 - byte)[:, None, :]).reshape(n, m).astype(np.float32).astype(ml_dtypes.float8_e4m3fn).view(np.uint8)
    words = codes.reshape(n // 512, 128, 4, m).transpose(0, 1, 3, 2)
    return np.ascontiguousarray(words), np.ascontiguousarray(byte.astype(np.uint8).reshape(n // 512, 16, m))


def relu(v):
    return np.maximum(v, 0.0)


def sigmoid(v):
    return 1.0 / (1.0 + np.exp(-np.maximum(v, -700.0)))


K, T, S, H, N = 1024, 2048, 512, 512, 512


def setup_inputs():
    n = np.random.standard_normal
    s = mx_kscale(K)[:, None]
    u = mx_kscale(H)
    packed_xT = pack_weight(n((K, T)) * s)
    packed_w1 = pack_fp4(n((K, N)) / np.sqrt(2 * K) / s)
    packed_w2 = pack_fp4(n((K, N)) / np.sqrt(2 * K) / s)
    packed_w5 = pack_fp4(n((H, N)) / np.sqrt(H) / u[:, None])
    return {
        "x_words": packed_xT[0],
        "x_scales": packed_xT[1],
        "w1_words": packed_w1[0],
        "w1_scales": packed_w1[1],
        "w2_words": packed_w2[0],
        "w2_scales": packed_w2[1],
        "w3": (n((K, H)) / np.sqrt(2 * K) / s * u).astype(np.float32),
        "w4": (n((K, H)) / np.sqrt(2 * K) / s * u).astype(np.float32),
        "w5_words": packed_w5[0],
        "w5_scales": packed_w5[1],
        "offs": striped(np.random.permutation(T)[:S]),
        "prev": striped(np.random.permutation(T)[:S]),
    }


def reference(x_words, x_scales, w1_words, w1_scales, w2_words, w2_scales, w3, w4, w5_words, w5_scales, offs, prev):
    xq = unpack_weight(x_words, x_scales)[:, unstriped(offs)]
    x_prev = unpack_weight(x_words, x_scales)[:, unstriped(prev)]
    h = relu(mxq(f64(w3), 0, "e4m3").T @ xq + mxq(f64(w4), 0, "e4m3").T @ x_prev)
    y = unpack_fp4(w5_words, w5_scales).T @ mxq(h, 0, "e4m3")
    r = sigmoid(unpack_fp4(w1_words, w1_scales).T @ xq + unpack_fp4(w2_words, w2_scales).T @ x_prev)
    out_0 = y * r
    return (out_0,) + planes(out_0)

@@ -1,0 +1,313 @@
+from contextlib import ExitStack
+
+import concourse.mybir as mybir
+from concourse.masks import make_identity
+
+K, T, S, H, N = 1024, 2048, 512, 512, 512
+FLOPS = 2 * S * (2 * K * N + 2 * K * H + H * N)
+
+F32 = mybir.dt.float32
+BF16 = mybir.dt.bfloat16
+I32 = mybir.dt.int32
+U32 = mybir.dt.uint32
+U16 = mybir.dt.uint16
+U8 = mybir.dt.uint8
+FP8X4 = mybir.dt.float8_e4m3fn_x4
+FP4X4 = mybir.dt.float4_e2m1fn_x4
+ACT = mybir.ActivationFunctionType
+ALU = mybir.AluOpType
+
+P = 128
+PACK = 4
+PASSES = 2
+CH = 128
+NCH = S // CH
+
+
+def tile_picked_zshift_relu_po_kernel(
+    tc, x_words, x_scales, w1_words, w1_scales, w2_words, w2_scales, w3, w4, w5_words, w5_scales, offs, prev, out_0, out_1, out_2
+):
+    nc = tc.nc
+    with ExitStack() as ctx:
+        keep = ctx.enter_context(tc.tile_pool(name="keep", bufs=1))
+        psum = ctx.enter_context(tc.psum_pool(name="psum", bufs=1))
+
+        def sb(name, shape, dtype, tag=None):
+            return keep.tile(shape, dtype, name=name, tag=tag or name, align_bytes=64)
+
+        lists = [keep.tile([P, S // 16], U16, name="offs_sb"), keep.tile([P, S // 16], U16, name="prev_sb")]
+        xs_win = sb("xs_win", [P, T], U8)
+        xw_win = {}
+        fp4 = [(w1_words, w1_scales, 2), (w2_words, w2_scales, 2), (w5_words, w5_scales, 1)]
+        w5_dealt = sb("w5_dealt", [P, 2 * N], U8)
+        s5_dealt = sb("s5_dealt", [P, N], U8)
+        ident = sb("ident", [P, P], F32)
+        xs_g = sb("xs_g", [P, 2 * S], U8)
+        xs_g1 = sb("xs_g1", [P, 2 * S], U8)
+        xw_g = [[sb(f"xw_g{a}{g}", [P, S], U32) for g in range(PASSES)] for a in range(2)]
+
+        warm_in = sb("warm_in", [P, 1], F32)
+        warm_out = sb("warm_out", [P, 1], F32)
+        nc.gpsimd.memset(warm_in[:], 0.0)
+        nc.scalar.activation(warm_out[:], warm_in[:], ACT.Sigmoid)
+
+        nc.vector.memset(xs_win[:].bitcast(I32), 0)
+        nc.vector.memset(xs_g1[:].bitcast(I32), 0)
+        make_identity(nc, ident[:])
+
+        fw12 = sb("fw12", [P, 2 * 2 * 2 * N], U8, "warm_out")
+        fw = [fw12[:, : 4 * N], fw12[:, 4 * N :], sb("fw2", [P, 2 * N], U8)[:]]
+
+        def load_fp4_words(a):
+            w, s, g = fp4[a]
+            nc.sync.dma_start(
+                out=fw[a].bitcast(I32).rearrange("p (g c) -> p g c", g=g),
+                in_=w.bitcast(I32).rearrange("g p c -> p g c"),
+            )
+
+        def load_fp4_scales(fs_all, a):
+            w, s, g = fp4[a]
+            nc.scalar.dma_start(
+                out=fs_all[0:16, 2 * N * a : 2 * N * a + g * N].bitcast(I32).rearrange("p (g c) -> p g c", g=g),
+                in_=s.bitcast(I32).rearrange("g r c -> r g c"),
+            )
+
+        def load_x_scales(eng):
+            for q in range(4):
+                eng.dma_start(
+                    out=xs_win[32 * q : 32 * q + 8, :].bitcast(I32),
+                    in_=x_scales.bitcast(I32)[:, 4 * q : 4 * q + 4, :],
+                )
+
+        def load_x_words(g, tag=None):
+            xw_win[g] = sb(f"xw_win{g}", [P, T], U32, tag)
+            nc.sync.dma_start(
+                out=xw_win[g][:].bitcast(I32),
+                in_=x_words[g].rearrange("p n t -> p (n t)").bitcast(I32),
+            )
+
+        wsrc = [w3, w4]
+        HALF = H // 2
+        w_raw = {}
+
+        def load_w(a, g, tag=None, split=False):
+            rows = wsrc[a][512 * g : 512 * (g + 1), :]
+            if split:
+                t = sb(f"w_raw{a}{g}", [P, 2, PACK, HALF], F32, tag)
+                for half in range(2):
+                    w_raw[(a, g, half)] = t[:, half, :, :]
+                    nc.sync.dma_start(
+                        out=t[:, half, :, :],
+                        in_=rows[:, HALF * half : HALF * (half + 1)].rearrange("(p j) c -> p j c", j=PACK),
+                    )
+            else:
+                t = sb(f"w_raw{a}{g}", [P, PACK, H], F32, tag)
+                for half in range(2):
+                    w_raw[(a, g, half)] = t[:, :, HALF * half : HALF * (half + 1)]
+                nc.sync.dma_start(out=t[:], in_=rows.rearrange("(p j) c -> p j c", j=PACK))
+
+        nc.sync.dma_start(lists[0][:], offs)
+        nc.sync.dma_start(lists[1][:], prev)
+        for half in range(2):
+            first = sb(f"w_first{half}", [P, PACK, HALF], F32)
+            w_raw[(0, 0, half)] = first[:]
+            nc.sync.dma_start(
+                out=first[:], in_=w3[0:512, HALF * half : HALF * (half + 1)].rearrange("(p j) c -> p j c", j=PACK)
+            )
+        load_fp4_words(2)
+        load_x_words(0)
+        load_x_scales(nc.scalar)
+        load_fp4_words(0)
+        load_fp4_words(1)
+
+        def deal_w5_words():
+            nc.vector.tensor_copy(
+                out=w5_dealt[:].rearrange("p (t m b) -> p t m b", t=PACK, b=2),
+                in_=fw[2].rearrange("p (m t b) -> p t m b", t=PACK, b=2),
+            )
+
+        def deal_w5_scales():
+            nc.vector.tensor_copy(
+                out=s5_dealt[:].rearrange("p (t m) -> p t m", t=PACK),
+                in_=fs[2].rearrange("p (m t) -> p t m", t=PACK),
+            )
+
+        def gather_words(a, g):
+            nc.vector.tensor_copy(xw_g[a][g][:], xw_win[g][:].indirect(lists[a][:]))
+
+        w_bf = {}
+        w_codes = {}
+        w_scales = {}
+
+        def cast_w(a, g, half, on_vector):
+            if (a, g) not in w_bf:
+                w_bf[(a, g)] = sb(f"w_bf{a}{g}", [P, PACK * H], BF16)
+            dst = w_bf[(a, g)][:].rearrange("p (t m j) -> p m j t", t=PACK, j=PACK)[:, 64 * half : 64 * (half + 1), :, :]
+            src = w_raw[(a, g, half)].rearrange("p j (m t) -> p m j t", t=PACK)
+            if on_vector:
+                nc.vector.tensor_copy(out=dst, in_=src)
+            else:
+                nc.scalar.copy(out=dst, in_=src)
+
+        def quantize_w(a, g, pieces):
+            w_codes[(a, g)] = sb(f"w_codes{a}{g}", [P, H], U32)
+            w_scales[(a, g)] = sb(f"w_scales{a}{g}", [P, H], U8)
+            wd = H // pieces
+            for u in range(pieces):
+                nc.vector.quantize_mx(
+                    out=w_codes[(a, g)][:, wd * u : wd * (u + 1)].bitcast(FP8X4),
+                    scales=w_scales[(a, g)][:, wd * u : wd * (u + 1)],
+                    in_=w_bf[(a, g)][:, PACK * wd * u : PACK * wd * (u + 1)],
+                )
+
+        r_ps = [psum.tile([P, N], F32, name=f"r_ps{c}", tag=f"rbank{c}") for c in range(NCH)]
+
+        def r_chunk(c):
+            for a, g in [(0, 0), (1, 0), (0, 1), (1, 1)]:
+                plane = xs_g if g == 0 else xs_g1
+                nc.tensor.matmul_mx(
+                    out=r_ps[c][:],
+                    lhsT=xw_g[a][g][:, CH * c : CH * (c + 1)].bitcast(FP8X4),
+                    lhsT_scale=plane[:, S * a + CH * c : S * a + CH * (c + 1)],
+                    rhs=fw[a][:, 2 * N * g : 2 * N * (g + 1)].bitcast(FP4X4),
+                    rhs_scale=fs[a][:, N * g : N * (g + 1)],
+                    start=(a == 0 and g == 0),
+                    stop=(a == 1 and g == 1),
+                )
+
+        sig = {}
+
+        def gate(c):
+            sig_t = sb(f"sig_t{c}", [P, PACK, P], F32)
+            nc.scalar.activation(sig_t[:], r_ps[c][:].rearrange("p (m t) -> p t m", t=PACK), ACT.Sigmoid)
+            turned = psum.tile([P, PACK, CH], F32, name=f"turned{c}", tag=f"rbank{c}")
+            for t in range(PACK):
+                nc.tensor.transpose(turned[:, t, :], sig_t[:, t, :], ident[:])
+            sig[c] = sb(f"sig{c}", [P, PACK, CH], F32)
+            nc.scalar.copy(sig[c][:], turned[:])
+
+        cast_w(0, 0, 0, True)
+        fs_all = sb("fs_all", [P, 5 * N], U8, "w_first0")
+        fs = [fs_all[:, 2 * N * a : 2 * N * a + g * N] for a, (w, s, g) in enumerate(fp4)]
+        nc.vector.memset(fs_all[:].bitcast(I32), 0)
+        for a in range(3):
+            load_fp4_scales(fs_all, a)
+        for q in range(1, 4):
+            nc.scalar.dma_start(
+                out=fs_all[32 * q : 32 * q + 4, :].bitcast(I32), in_=fs_all[4 * q : 4 * q + 4, :].bitcast(I32)
+            )
+        cast_w(0, 0, 1, False)
+        deal_w5_words()
+        load_x_words(1, "fw2")
+        for a in range(2):
+            nc.vector.tensor_copy(xs_g[:, S * a : S * (a + 1)], xs_win[:].indirect(lists[a][:]))
+        load_w(1, 0, "xs_win")
+        nc.scalar.dma_start(out=xs_g1[0:112, :].bitcast(I32), in_=xs_g[4:116, :].bitcast(I32))
+        gather_words(0, 0)
+        gather_words(1, 0)
+        load_w(0, 1, "xw_win0")
+        quantize_w(0, 0, 1)
+        gather_words(0, 1)
+        gather_words(1, 1)
+        load_w(1, 1, "fw2", True)
+        for c in range(NCH):
+            r_chunk(c)
+        deal_w5_scales()
+        cast_w(1, 0, 0, False)
+        cast_w(1, 0, 1, False)
+        cast_w(0, 1, 0, True)
+        quantize_w(1, 0, 1)
+        cast_w(0, 1, 1, True)
+        cast_w(1, 1, 0, True)
+        quantize_w(0, 1, 1)
+        cast_w(1, 1, 1, True)
+        quantize_w(1, 1, 2)
+        for c in range(NCH):
+            gate(c)
+
+        o_codes = sb("o_codes", [P, S], U32)
+        o_scales = sb("o_scales", [P, S], U8)
+        out_v = out_0.rearrange("(p t) n -> p t n", t=PACK)
+        order = [(0, 0), (1, 0), (0, 1), (1, 1)]
+        st = {}
+
+        def h_mm(c):
+            cols = slice(CH * c, CH * (c + 1))
+            h_ps = psum.tile([P, PACK, CH], F32, name=f"h_ps{c}", tag=f"bank{c}")
+            for t in range(PACK):
+                for i, (a, g) in enumerate(order):
+                    nc.tensor.matmul_mx(
+                        out=h_ps[:, t, :],
+                        lhsT=w_codes[(a, g)][:, P * t : P * (t + 1)].bitcast(FP8X4),
+                        lhsT_scale=w_scales[(a, g)][:, P * t : P * (t + 1)],
+                        rhs=xw_g[a][g][:, cols].bitcast(FP8X4),
+                        rhs_scale=xs_g[4 * g : P, S * a + CH * c : S * a + CH * (c + 1)],
+                        start=(i == 0),
+                        stop=(i == 3),
+                    )
+            st[("h", c)] = h_ps
+
+        def h_quant(c):
+            h_bf = sb(f"h_bf{c}", [P, CH * PACK], BF16)
+            nc.scalar.activation(
+                h_bf[:].rearrange("p (n t) -> p n t", t=PACK), st[("h", c)][:].rearrange("p t n -> p n t"), ACT.Relu
+            )
+            h_codes = sb(f"h_codes{c}", [P, CH], U32)
+            h_scales = sb(f"h_scales{c}", [P, CH], U8)
+            nc.vector.quantize_mx(out=h_codes[:].bitcast(FP8X4), scales=h_scales[:], in_=h_bf[:])
+            st[("hq", c)] = (h_codes, h_scales)
+
+        def y_mm(c):
+            h_codes, h_scales = st[("hq", c)]
+            y_ps = psum.tile([P, PACK, CH], F32, name=f"y_ps{c}", tag=f"bank{c}")
+            for t in range(PACK):
+                nc.tensor.matmul_mx(
+                    out=y_ps[:, t, :],
+                    lhsT=w5_dealt[:, 2 * P * t : 2 * P * (t + 1)].bitcast(FP4X4),
+                    lhsT_scale=s5_dealt[:, P * t : P * (t + 1)],
+                    rhs=h_codes[:].bitcast(FP8X4),
+                    rhs_scale=h_scales[:],
+                    start=True,
+                    stop=True,
+                )
+            st[("y", c)] = y_ps
+
+        def finish(c):
+            cols = slice(CH * c, CH * (c + 1))
+            o = sb(f"o{c}", [P, PACK, CH], F32)
+            nc.vector.tensor_tensor(o[:], st[("y", c)][:], sig[c][:], ALU.mult)
+            nc.sync.dma_start(out=out_v[:, :, cols], in_=o[:])
+            st[("o", c)] = o
+
+        def cast_o(c):
+            o_bf = sb(f"o_bf{c}", [P, CH * PACK], BF16)
+            nc.scalar.copy(
+                out=o_bf[:].rearrange("p (c i t) -> p c t i", i=4, t=PACK),
+                in_=st[("o", c)][:].rearrange("p t (c i) -> p c t i", i=4),
+            )
+            st[("obf", c)] = o_bf
+
+        def quant_o(c):
+            cols = slice(CH * c, CH * (c + 1))
+            nc.vector.quantize_mx(out=o_codes[:, cols].bitcast(FP8X4), scales=o_scales[:, cols], in_=st[("obf", c)][:])
+            nc.sync.dma_start(
+                out=out_1[0].rearrange("p n t -> p (n t)").bitcast(I32)[:, cols], in_=o_codes[:, cols].bitcast(I32)
+            )
+
+        for step in range(NCH + 3):
+            if step < NCH:
+                h_mm(step)
+            if 1 <= step < NCH + 1:
+                h_quant(step - 1)
+                y_mm(step - 1)
+            if 2 <= step < NCH + 2:
+                finish(step - 2)
+            if 3 <= step:
+                quant_o(step - 3)
+            if 2 <= step < NCH + 2:
+                cast_o(step - 2)
+        for q in range(4):
+            eng = nc.scalar if q % 2 else nc.sync
+            eng.dma_start(
+                out=out_2[0].bitcast(I32)[4 * q : 4 * q + 4, :], in_=o_scales[32 * q : 32 * q + 4, :].bitcast(I32)
+            )

@@ -40,23 +40,24 @@ def tile_picked_zshift_relu_po_kernel(
         xw_win = {}
         fp4 = [(w1_words, w1_scales, 2), (w2_words, w2_scales, 2), (w5_words, w5_scales, 1)]
         w5_dealt = sb("w5_dealt", [P, 2 * N], U8)
-        s5_dealt = sb("s5_dealt", [P, N], U8)
         ident = sb("ident", [P, P], F32)
         xs_g = sb("xs_g", [P, 2 * S], U8)
         xs_g1 = sb("xs_g1", [P, 2 * S], U8)
         xw_g = [[sb(f"xw_g{a}{g}", [P, S], U32) for g in range(PASSES)] for a in range(2)]
 
-        warm_in = sb("warm_in", [P, 1], F32)
-        warm_out = sb("warm_out", [P, 1], F32)
-        nc.gpsimd.memset(warm_in[:], 0.0)
-        nc.scalar.activation(warm_out[:], warm_in[:], ACT.Sigmoid)
-
+        fs_all = sb("fs_all", [P, 4 * N], U8)
         nc.vector.memset(xs_win[:].bitcast(I32), 0)
+        nc.vector.memset(fs_all[:].bitcast(I32), 0)
+        warm_in = sb("warm_in", [P, 1], F32)
+        warm_bias = sb("warm_bias", [P, 1], F32)
+        warm_out = sb("warm_out", [P, 1], F32)
+        nc.vector.memset(warm_in[:], 0.0)
+        nc.vector.memset(warm_bias[:], 0.0)
+        nc.scalar.activation(warm_out[:], warm_in[:], ACT.Sigmoid, bias=warm_bias[:])
         nc.vector.memset(xs_g1[:].bitcast(I32), 0)
         make_identity(nc, ident[:])
 
-        fw12 = sb("fw12", [P, 2 * 2 * 2 * N], U8, "warm_out")
-        fw = [fw12[:, : 4 * N], fw12[:, 4 * N :], sb("fw2", [P, 2 * N], U8)[:]]
+        fw = {}
 
         def load_fp4_words(a):
             w, s, g = fp4[a]
@@ -65,18 +66,18 @@ def tile_picked_zshift_relu_po_kernel(
                 in_=w.bitcast(I32).rearrange("g p c -> p g c"),
             )
 
-        def load_fp4_scales(fs_all, a):
+        def load_fp4_scales(dst, a):
             w, s, g = fp4[a]
-            nc.scalar.dma_start(
-                out=fs_all[0:16, 2 * N * a : 2 * N * a + g * N].bitcast(I32).rearrange("p (g c) -> p g c", g=g),
+            nc.sync.dma_start(
+                out=dst.bitcast(I32).rearrange("p (g c) -> p g c", g=g),
                 in_=s.bitcast(I32).rearrange("g r c -> r g c"),
             )
 
         def load_x_scales(eng):
-            for q in range(4):
+            for r in range(4):
                 eng.dma_start(
-                    out=xs_win[32 * q : 32 * q + 8, :].bitcast(I32),
-                    in_=x_scales.bitcast(I32)[:, 4 * q : 4 * q + 4, :],
+                    out=xs_win[r:P:16, :].bitcast(I32),
+                    in_=x_scales.bitcast(I32)[:, r:16:4, :].rearrange("g q c -> q g c"),
                 )
 
         def load_x_words(g, tag=None):
@@ -90,46 +91,37 @@ def tile_picked_zshift_relu_po_kernel(
         HALF = H // 2
         w_raw = {}
 
-        def load_w(a, g, tag=None, split=False):
-            rows = wsrc[a][512 * g : 512 * (g + 1), :]
-            if split:
-                t = sb(f"w_raw{a}{g}", [P, 2, PACK, HALF], F32, tag)
-                for half in range(2):
-                    w_raw[(a, g, half)] = t[:, half, :, :]
-                    nc.sync.dma_start(
-                        out=t[:, half, :, :],
-                        in_=rows[:, HALF * half : HALF * (half + 1)].rearrange("(p j) c -> p j c", j=PACK),
-                    )
-            else:
-                t = sb(f"w_raw{a}{g}", [P, PACK, H], F32, tag)
-                for half in range(2):
-                    w_raw[(a, g, half)] = t[:, :, HALF * half : HALF * (half + 1)]
-                nc.sync.dma_start(out=t[:], in_=rows.rearrange("(p j) c -> p j c", j=PACK))
+        def load_w(a, g, lo, hi, dst):
+            rows = wsrc[a][512 * g : 512 * (g + 1), lo:hi]
+            dst = dst.rearrange("p (j c) -> p j c", j=PACK)
+            nc.sync.dma_start(out=dst, in_=rows.rearrange("(p j) c -> p j c", j=PACK))
+            return dst
+
+        fs = [fs_all[:, : 2 * N], fs_all[:, 2 * N :]]
+        s5_raw = sb("s5_raw", [P, N], U8)
+        nc.gpsimd.memset(s5_raw[:].bitcast(I32), 0)
 
         nc.sync.dma_start(lists[0][:], offs)
         nc.sync.dma_start(lists[1][:], prev)
-        for half in range(2):
-            first = sb(f"w_first{half}", [P, PACK, HALF], F32)
-            w_raw[(0, 0, half)] = first[:]
-            nc.sync.dma_start(
-                out=first[:], in_=w3[0:512, HALF * half : HALF * (half + 1)].rearrange("(p j) c -> p j c", j=PACK)
-            )
-        load_fp4_words(2)
         load_x_words(0)
-        load_x_scales(nc.scalar)
-        load_fp4_words(0)
-        load_fp4_words(1)
+        load_x_scales(nc.sync)
+        load_fp4_scales(fs[0][0:16, :], 0)
+        load_fp4_scales(fs[1][0:16, :], 1)
+        for q in range(4):
+            nc.gpsimd.dma_start(
+                out=s5_raw[32 * q : 32 * q + 4, :].bitcast(I32), in_=w5_scales[0].bitcast(I32)[4 * q : 4 * q + 4, :]
+            )
+        load_x_words(1, "warm_out")
+        fw_all = sb("fw_all", [P, 5 * 2 * N], U8, "warm_in")
+        for a in range(3):
+            fw[a] = fw_all[:, 4 * N * a : 4 * N * a + 2 * N * fp4[a][2]]
+            load_fp4_words(a)
+        w_raw[(0, 0, 0)] = load_w(0, 0, 0, HALF, sb("w_raw00a", [P, PACK * HALF], F32, "warm_bias")[:])
 
         def deal_w5_words():
             nc.vector.tensor_copy(
                 out=w5_dealt[:].rearrange("p (t m b) -> p t m b", t=PACK, b=2),
                 in_=fw[2].rearrange("p (m t b) -> p t m b", t=PACK, b=2),
-            )
-
-        def deal_w5_scales():
-            nc.vector.tensor_copy(
-                out=s5_dealt[:].rearrange("p (t m) -> p t m", t=PACK),
-                in_=fs[2].rearrange("p (m t) -> p t m", t=PACK),
             )
 
         def gather_words(a, g):
@@ -139,26 +131,25 @@ def tile_picked_zshift_relu_po_kernel(
         w_codes = {}
         w_scales = {}
 
-        def cast_w(a, g, half, on_vector):
+        def cast_w(a, g, lo, hi, on_vector):
             if (a, g) not in w_bf:
                 w_bf[(a, g)] = sb(f"w_bf{a}{g}", [P, PACK * H], BF16)
-            dst = w_bf[(a, g)][:].rearrange("p (t m j) -> p m j t", t=PACK, j=PACK)[:, 64 * half : 64 * (half + 1), :, :]
-            src = w_raw[(a, g, half)].rearrange("p j (m t) -> p m j t", t=PACK)
+            dst = w_bf[(a, g)][:, PACK * lo : PACK * hi].rearrange("p (c i j) -> p c j i", i=4, j=PACK)
+            src = w_raw[(a, g, lo)].rearrange("p j (c i) -> p c j i", i=4)
             if on_vector:
                 nc.vector.tensor_copy(out=dst, in_=src)
             else:
                 nc.scalar.copy(out=dst, in_=src)
 
-        def quantize_w(a, g, pieces):
-            w_codes[(a, g)] = sb(f"w_codes{a}{g}", [P, H], U32)
-            w_scales[(a, g)] = sb(f"w_scales{a}{g}", [P, H], U8)
-            wd = H // pieces
-            for u in range(pieces):
-                nc.vector.quantize_mx(
-                    out=w_codes[(a, g)][:, wd * u : wd * (u + 1)].bitcast(FP8X4),
-                    scales=w_scales[(a, g)][:, wd * u : wd * (u + 1)],
-                    in_=w_bf[(a, g)][:, PACK * wd * u : PACK * wd * (u + 1)],
-                )
+        def quantize_w(a, g, lo, hi):
+            if (a, g) not in w_codes:
+                w_codes[(a, g)] = sb(f"w_codes{a}{g}", [P, H], U32)
+                w_scales[(a, g)] = sb(f"w_scales{a}{g}", [P, H], U8)
+            nc.vector.quantize_mx(
+                out=w_codes[(a, g)][:, lo:hi].bitcast(FP8X4),
+                scales=w_scales[(a, g)][:, lo:hi],
+                in_=w_bf[(a, g)][:, PACK * lo : PACK * hi],
+            )
 
         r_ps = [psum.tile([P, N], F32, name=f"r_ps{c}", tag=f"rbank{c}") for c in range(NCH)]
 
@@ -178,50 +169,54 @@ def tile_picked_zshift_relu_po_kernel(
         sig = {}
 
         def gate(c):
-            sig_t = sb(f"sig_t{c}", [P, PACK, P], F32)
-            nc.scalar.activation(sig_t[:], r_ps[c][:].rearrange("p (m t) -> p t m", t=PACK), ACT.Sigmoid)
+            sig_t = rest[:, N * c : N * (c + 1)].rearrange("p (t m) -> p t m", t=PACK)
+            nc.scalar.activation(sig_t, r_ps[c][:].rearrange("p (m t) -> p t m", t=PACK), ACT.Sigmoid)
             turned = psum.tile([P, PACK, CH], F32, name=f"turned{c}", tag=f"rbank{c}")
             for t in range(PACK):
                 nc.tensor.transpose(turned[:, t, :], sig_t[:, t, :], ident[:])
             sig[c] = sb(f"sig{c}", [P, PACK, CH], F32)
             nc.scalar.copy(sig[c][:], turned[:])
 
-        cast_w(0, 0, 0, True)
-        fs_all = sb("fs_all", [P, 5 * N], U8, "w_first0")
-        fs = [fs_all[:, 2 * N * a : 2 * N * a + g * N] for a, (w, s, g) in enumerate(fp4)]
-        nc.vector.memset(fs_all[:].bitcast(I32), 0)
-        for a in range(3):
-            load_fp4_scales(fs_all, a)
+        gather_words(0, 0)
+        gather_words(1, 0)
+        w_raw[(0, 0, HALF)] = load_w(0, 0, HALF, H, sb("w_raw00b", [P, PACK * HALF], F32, "xw_win0")[:])
         for q in range(1, 4):
             nc.scalar.dma_start(
                 out=fs_all[32 * q : 32 * q + 4, :].bitcast(I32), in_=fs_all[4 * q : 4 * q + 4, :].bitcast(I32)
             )
-        cast_w(0, 0, 1, False)
-        deal_w5_words()
-        load_x_words(1, "fw2")
         for a in range(2):
             nc.vector.tensor_copy(xs_g[:, S * a : S * (a + 1)], xs_win[:].indirect(lists[a][:]))
-        load_w(1, 0, "xs_win")
-        nc.scalar.dma_start(out=xs_g1[0:112, :].bitcast(I32), in_=xs_g[4:116, :].bitcast(I32))
-        gather_words(0, 0)
-        gather_words(1, 0)
-        load_w(0, 1, "xw_win0")
-        quantize_w(0, 0, 1)
+        nc.scalar.dma_start(out=xs_g1[0:112, :].bitcast(I32), in_=xs_g[16:128, :].bitcast(I32))
+        rest = sb("w_rest", [P, 3 * PACK * H], F32, "xs_win")
+        pieces = [(1, 0, 0, 256), (1, 0, 256, 512), (0, 1, 0, 256), (0, 1, 256, 512), (1, 1, 0, 256), (1, 1, 256, 384), (1, 1, 384, 512)]
+        at = 0
+        for a, g, lo, hi in pieces:
+            w_raw[(a, g, lo)] = load_w(a, g, lo, hi, rest[:, at : at + PACK * (hi - lo)])
+            at = at + PACK * (hi - lo)
         gather_words(0, 1)
         gather_words(1, 1)
-        load_w(1, 1, "fw2", True)
         for c in range(NCH):
             r_chunk(c)
-        deal_w5_scales()
-        cast_w(1, 0, 0, False)
-        cast_w(1, 0, 1, False)
-        cast_w(0, 1, 0, True)
-        quantize_w(1, 0, 1)
-        cast_w(0, 1, 1, True)
-        cast_w(1, 1, 0, True)
-        quantize_w(0, 1, 1)
-        cast_w(1, 1, 1, True)
-        quantize_w(1, 1, 2)
+        deal_w5_words()
+        s5_dealt = sb("s5_dealt", [P, N], U8, "xw_win1")
+        nc.vector.tensor_copy(
+            out=s5_dealt[:].rearrange("p (t m) -> p t m", t=PACK), in_=s5_raw[:].rearrange("p (m t) -> p t m", t=PACK)
+        )
+        cast_w(0, 0, 0, 256, False)
+        cast_w(0, 0, 256, 512, False)
+        quantize_w(0, 0, 0, H)
+        cast_w(1, 0, 0, 256, False)
+        cast_w(1, 0, 256, 512, True)
+        quantize_w(1, 0, 0, H)
+        cast_w(0, 1, 0, 256, True)
+        cast_w(0, 1, 256, 512, True)
+        quantize_w(0, 1, 0, H)
+        cast_w(1, 1, 0, 256, True)
+        cast_w(1, 1, 256, 384, True)
+        quantize_w(1, 1, 0, 256)
+        cast_w(1, 1, 384, 512, True)
+        quantize_w(1, 1, 256, 384)
+        quantize_w(1, 1, 384, 512)
         for c in range(NCH):
             gate(c)
 
@@ -232,25 +227,32 @@ def tile_picked_zshift_relu_po_kernel(
         st = {}
 
         def h_mm(c):
-            cols = slice(CH * c, CH * (c + 1))
-            h_ps = psum.tile([P, PACK, CH], F32, name=f"h_ps{c}", tag=f"bank{c}")
-            for t in range(PACK):
-                for i, (a, g) in enumerate(order):
-                    nc.tensor.matmul_mx(
-                        out=h_ps[:, t, :],
-                        lhsT=w_codes[(a, g)][:, P * t : P * (t + 1)].bitcast(FP8X4),
-                        lhsT_scale=w_scales[(a, g)][:, P * t : P * (t + 1)],
-                        rhs=xw_g[a][g][:, cols].bitcast(FP8X4),
-                        rhs_scale=xs_g[4 * g : P, S * a + CH * c : S * a + CH * (c + 1)],
-                        start=(i == 0),
-                        stop=(i == 3),
-                    )
+            h_ps = psum.tile([P, H], F32, name=f"h_ps{c}", tag=f"bank{c}")
+            for i, (a, g) in enumerate(order):
+                nc.tensor.matmul_mx(
+                    out=h_ps[:],
+                    lhsT=xw_g[a][g][:, CH * c : CH * (c + 1)].bitcast(FP8X4),
+                    lhsT_scale=(xs_g if g == 0 else xs_g1)[:, S * a + CH * c : S * a + CH * (c + 1)],
+                    rhs=w_codes[(a, g)][:].bitcast(FP8X4),
+                    rhs_scale=w_scales[(a, g)][:],
+                    start=(i == 0),
+                    stop=(i == 3),
+                )
             st[("h", c)] = h_ps
 
         def h_quant(c):
-            h_bf = sb(f"h_bf{c}", [P, CH * PACK], BF16)
+            h_t = sb(f"h_t{c}", [P, H], BF16)
             nc.scalar.activation(
-                h_bf[:].rearrange("p (n t) -> p n t", t=PACK), st[("h", c)][:].rearrange("p t n -> p n t"), ACT.Relu
+                h_t[:].rearrange("p (u m e) -> p u m e", u=2, e=2),
+                st[("h", c)][:].rearrange("p (m u e) -> p u m e", u=2, e=2),
+                ACT.Relu,
+            )
+            pairs = psum.tile([P, 2, CH], F32, name=f"pairs{c}", tag=f"bank{c}")
+            for u in range(2):
+                nc.tensor.transpose(pairs[:, u, :], h_t[:].bitcast(F32)[:, P * u : P * (u + 1)], ident[:])
+            h_bf = sb(f"h_bf{c}", [P, CH * PACK], BF16)
+            nc.vector.tensor_copy(
+                out=h_bf[:].bitcast(F32).rearrange("p (n u) -> p n u", u=2), in_=pairs[:].rearrange("p u n -> p n u")
             )
             h_codes = sb(f"h_codes{c}", [P, CH], U32)
             h_scales = sb(f"h_scales{c}", [P, CH], U8)
@@ -294,18 +296,17 @@ def tile_picked_zshift_relu_po_kernel(
                 out=out_1[0].rearrange("p n t -> p (n t)").bitcast(I32)[:, cols], in_=o_codes[:, cols].bitcast(I32)
             )
 
-        for step in range(NCH + 3):
+        for c in range(NCH):
+            h_mm(c)
+        for step in range(NCH + 2):
             if step < NCH:
-                h_mm(step)
+                h_quant(step)
+                y_mm(step)
             if 1 <= step < NCH + 1:
-                h_quant(step - 1)
-                y_mm(step - 1)
-            if 2 <= step < NCH + 2:
-                finish(step - 2)
-            if 3 <= step:
-                quant_o(step - 3)
-            if 2 <= step < NCH + 2:
-                cast_o(step - 2)
+                finish(step - 1)
+                cast_o(step - 1)
+            if 2 <= step:
+                quant_o(step - 2)
         for q in range(4):
             eng = nc.scalar if q % 2 else nc.sync
             eng.dma_start(

@@ -46,8 +46,8 @@ def tile_picked_zshift_relu_po_kernel(
         xw_g = [[sb(f"xw_g{a}{g}", [P, S], U32) for g in range(PASSES)] for a in range(2)]
 
         fs_all = sb("fs_all", [P, 4 * N], U8)
-        nc.vector.memset(xs_win[:].bitcast(I32), 0)
         nc.vector.memset(fs_all[:].bitcast(I32), 0)
+        nc.vector.memset(xs_win[:].bitcast(I32), 0)
         warm_in = sb("warm_in", [P, 1], F32)
         warm_bias = sb("warm_bias", [P, 1], F32)
         warm_out = sb("warm_out", [P, 1], F32)
@@ -104,19 +104,18 @@ def tile_picked_zshift_relu_po_kernel(
         nc.sync.dma_start(lists[0][:], offs)
         nc.sync.dma_start(lists[1][:], prev)
         load_x_words(0)
-        load_x_scales(nc.sync)
         load_fp4_scales(fs[0][0:16, :], 0)
         load_fp4_scales(fs[1][0:16, :], 1)
+        load_x_scales(nc.sync)
         for q in range(4):
             nc.gpsimd.dma_start(
                 out=s5_raw[32 * q : 32 * q + 4, :].bitcast(I32), in_=w5_scales[0].bitcast(I32)[4 * q : 4 * q + 4, :]
             )
-        load_x_words(1, "warm_out")
+        load_x_words(1, "warm_bias")
         fw_all = sb("fw_all", [P, 5 * 2 * N], U8, "warm_in")
         for a in range(3):
             fw[a] = fw_all[:, 4 * N * a : 4 * N * a + 2 * N * fp4[a][2]]
             load_fp4_words(a)
-        w_raw[(0, 0, 0)] = load_w(0, 0, 0, HALF, sb("w_raw00a", [P, PACK * HALF], F32, "warm_bias")[:])
 
         def deal_w5_words():
             nc.vector.tensor_copy(
@@ -169,7 +168,7 @@ def tile_picked_zshift_relu_po_kernel(
         sig = {}
 
         def gate(c):
-            sig_t = rest[:, N * c : N * (c + 1)].rearrange("p (t m) -> p t m", t=PACK)
+            sig_t = rest[:, PACK * H + N * c : PACK * H + N * (c + 1)].rearrange("p (t m) -> p t m", t=PACK)
             nc.scalar.activation(sig_t, r_ps[c][:].rearrange("p (m t) -> p t m", t=PACK), ACT.Sigmoid)
             turned = psum.tile([P, PACK, CH], F32, name=f"turned{c}", tag=f"rbank{c}")
             for t in range(PACK):
@@ -179,14 +178,16 @@ def tile_picked_zshift_relu_po_kernel(
 
         gather_words(0, 0)
         gather_words(1, 0)
-        w_raw[(0, 0, HALF)] = load_w(0, 0, HALF, H, sb("w_raw00b", [P, PACK * HALF], F32, "xw_win0")[:])
+        first = sb("w_first", [P, PACK * H], F32, "xw_win0")
+        for lo in (0, HALF):
+            w_raw[(0, 0, lo)] = load_w(0, 0, lo, lo + HALF, first[:, PACK * lo : PACK * (lo + HALF)])
         for q in range(1, 4):
             nc.scalar.dma_start(
                 out=fs_all[32 * q : 32 * q + 4, :].bitcast(I32), in_=fs_all[4 * q : 4 * q + 4, :].bitcast(I32)
             )
         for a in range(2):
             nc.vector.tensor_copy(xs_g[:, S * a : S * (a + 1)], xs_win[:].indirect(lists[a][:]))
-        nc.scalar.dma_start(out=xs_g1[0:112, :].bitcast(I32), in_=xs_g[16:128, :].bitcast(I32))
+        nc.sync.dma_start(out=xs_g1[0:112, :].bitcast(I32), in_=xs_g[16:128, :].bitcast(I32))
         rest = sb("w_rest", [P, 3 * PACK * H], F32, "xs_win")
         pieces = [(1, 0, 0, 256), (1, 0, 256, 512), (0, 1, 0, 256), (0, 1, 256, 512), (1, 1, 0, 256), (1, 1, 256, 384), (1, 1, 384, 512)]
         at = 0
@@ -208,7 +209,7 @@ def tile_picked_zshift_relu_po_kernel(
         cast_w(1, 0, 0, 256, False)
         cast_w(1, 0, 256, 512, True)
         quantize_w(1, 0, 0, H)
-        cast_w(0, 1, 0, 256, True)
+        cast_w(0, 1, 0, 256, False)
         cast_w(0, 1, 256, 512, True)
         quantize_w(0, 1, 0, H)
         cast_w(1, 1, 0, 256, True)

@@ -53,7 +53,9 @@ def tile_picked_zshift_relu_po_kernel(
         warm_out = sb("warm_out", [P, 1], F32)
         nc.vector.memset(warm_in[:], 0.0)
         nc.vector.memset(warm_bias[:], 0.0)
-        nc.scalar.activation(warm_out[:], warm_in[:], ACT.Sigmoid, bias=warm_bias[:])
+        warm_scale = sb("warm_scale", [P, 1], F32)
+        nc.vector.memset(warm_scale[:], 0.0)
+        nc.scalar.activation(warm_out[:], warm_in[:], ACT.Sigmoid, bias=warm_bias[:], scale=warm_scale[:])
         nc.vector.memset(xs_g1[:].bitcast(I32), 0)
         make_identity(nc, ident[:])
 
@@ -116,6 +118,9 @@ def tile_picked_zshift_relu_po_kernel(
         for a in range(3):
             fw[a] = fw_all[:, 4 * N * a : 4 * N * a + 2 * N * fp4[a][2]]
             load_fp4_words(a)
+        first = load_w(0, 0, 0, H, sb("w_first", [P, PACK * H], F32, "warm_scale")[:])
+        for lo in (0, HALF):
+            w_raw[(0, 0, lo)] = first[:, :, lo : lo + HALF]
 
         def deal_w5_words():
             nc.vector.tensor_copy(
@@ -170,6 +175,10 @@ def tile_picked_zshift_relu_po_kernel(
         def gate(c):
             sig_t = rest[:, PACK * H + N * c : PACK * H + N * (c + 1)].rearrange("p (t m) -> p t m", t=PACK)
             nc.scalar.activation(sig_t, r_ps[c][:].rearrange("p (m t) -> p t m", t=PACK), ACT.Sigmoid)
+            sig[c] = sig_t
+
+        def turn_gate(c):
+            sig_t = sig[c]
             turned = psum.tile([P, PACK, CH], F32, name=f"turned{c}", tag=f"rbank{c}")
             for t in range(PACK):
                 nc.tensor.transpose(turned[:, t, :], sig_t[:, t, :], ident[:])
@@ -177,10 +186,6 @@ def tile_picked_zshift_relu_po_kernel(
             nc.scalar.copy(sig[c][:], turned[:])
 
         gather_words(0, 0)
-        gather_words(1, 0)
-        first = sb("w_first", [P, PACK * H], F32, "xw_win0")
-        for lo in (0, HALF):
-            w_raw[(0, 0, lo)] = load_w(0, 0, lo, lo + HALF, first[:, PACK * lo : PACK * (lo + HALF)])
         for q in range(1, 4):
             nc.scalar.dma_start(
                 out=fs_all[32 * q : 32 * q + 4, :].bitcast(I32), in_=fs_all[4 * q : 4 * q + 4, :].bitcast(I32)
@@ -194,6 +199,7 @@ def tile_picked_zshift_relu_po_kernel(
         for a, g, lo, hi in pieces:
             w_raw[(a, g, lo)] = load_w(a, g, lo, hi, rest[:, at : at + PACK * (hi - lo)])
             at = at + PACK * (hi - lo)
+        gather_words(1, 0)
         gather_words(0, 1)
         gather_words(1, 1)
         for c in range(NCH):
@@ -204,7 +210,7 @@ def tile_picked_zshift_relu_po_kernel(
             out=s5_dealt[:].rearrange("p (t m) -> p t m", t=PACK), in_=s5_raw[:].rearrange("p (m t) -> p t m", t=PACK)
         )
         cast_w(0, 0, 0, 256, False)
-        cast_w(0, 0, 256, 512, False)
+        cast_w(0, 0, 256, 512, True)
         quantize_w(0, 0, 0, H)
         cast_w(1, 0, 0, 256, False)
         cast_w(1, 0, 256, 512, True)
@@ -220,6 +226,8 @@ def tile_picked_zshift_relu_po_kernel(
         quantize_w(1, 1, 384, 512)
         for c in range(NCH):
             gate(c)
+        for c in range(NCH):
+            turn_gate(c)
 
         o_codes = sb("o_codes", [P, S], U32)
         o_scales = sb("o_scales", [P, S], U8)

@@ -1,7 +1,6 @@
 from contextlib import ExitStack
 
 import concourse.mybir as mybir
-from concourse.masks import make_identity
 
 K, T, S, H, N = 1024, 2048, 512, 512, 512
 FLOPS = 2 * S * (2 * K * N + 2 * K * H + H * N)
@@ -32,240 +31,247 @@ def tile_picked_zshift_relu_po_kernel(
         keep = ctx.enter_context(tc.tile_pool(name="keep", bufs=1))
         psum = ctx.enter_context(tc.psum_pool(name="psum", bufs=1))
 
+        shared = ctx.enter_context(tc.tile_pool(name="shared", bufs=1))
+
         def sb(name, shape, dtype, tag=None):
             return keep.tile(shape, dtype, name=name, tag=tag or name, align_bytes=64)
 
+        def placed(name, shape, dtype, offset):
+            return shared.tile(shape, dtype, name=name, align_bytes=64, offset=offset)
+
         lists = [keep.tile([P, S // 16], U16, name="offs_sb"), keep.tile([P, S // 16], U16, name="prev_sb")]
         xs_win = sb("xs_win", [P, T], U8)
-        xw_win = {}
-        fp4 = [(w1_words, w1_scales, 2), (w2_words, w2_scales, 2), (w5_words, w5_scales, 1)]
+        ones = sb("ones", [P, P], F32)
+        xw_win = [sb("xw_win0", [P, T], U32), placed("xw_win1", [P, T], U32, 4 * T + 8 * N + N)]
+        W5_AT = 4 * T + 8 * N
+        w5_raw = placed("w5_raw", [P, 2 * N], U8, W5_AT)
+        xs_g = [sb(f"xs_g{g}", [P, 2 * S], U8) for g in range(PASSES)]
+        xw_g = [[sb(f"xw_g{a}{g}", [P, S], U32) for g in range(PASSES)] for a in range(2)]
+        gate_words_all = placed("gate_words", [P, 2 * PASSES * 2 * N], U8, W5_AT + N - 8 * N)
+        gate_words = [gate_words_all[:, PASSES * 2 * N * a : PASSES * 2 * N * (a + 1)] for a in range(2)]
+        gate_scales = sb("gate_scales", [P, 2 * PASSES * N], U8)
+        s5_raw = sb("s5_raw", [P, N], U8)
         w5_dealt = sb("w5_dealt", [P, 2 * N], U8)
         ident = sb("ident", [P, P], F32)
-        xs_g = sb("xs_g", [P, 2 * S], U8)
-        xs_g1 = sb("xs_g1", [P, 2 * S], U8)
-        xw_g = [[sb(f"xw_g{a}{g}", [P, S], U32) for g in range(PASSES)] for a in range(2)]
-
-        fs_all = sb("fs_all", [P, 4 * N], U8)
-        nc.vector.memset(fs_all[:].bitcast(I32), 0)
-        nc.vector.memset(xs_win[:].bitcast(I32), 0)
-        warm_in = sb("warm_in", [P, 1], F32)
-        warm_bias = sb("warm_bias", [P, 1], F32)
         warm_out = sb("warm_out", [P, 1], F32)
-        nc.vector.memset(warm_in[:], 0.0)
-        nc.vector.memset(warm_bias[:], 0.0)
-        warm_scale = sb("warm_scale", [P, 1], F32)
-        nc.vector.memset(warm_scale[:], 0.0)
-        nc.scalar.activation(warm_out[:], warm_in[:], ACT.Sigmoid, bias=warm_bias[:], scale=warm_scale[:])
-        nc.vector.memset(xs_g1[:].bitcast(I32), 0)
-        make_identity(nc, ident[:])
 
-        fw = {}
+        nc.vector.memset(gate_scales[:].bitcast(I32), 0)
+        nc.vector.memset(xs_g[1][:].bitcast(I32), 0)
+        nc.vector.memset(s5_raw[:].bitcast(I32), 0)
+        nc.gpsimd.memset(xs_win[:].bitcast(I32), 0)
+        nc.gpsimd.memset(ones[:], 1.0)
+        nc.gpsimd.affine_select(
+            out=ident[:], in_=ones[:], compare_op=ALU.is_equal, fill=0.0, base=0, pattern=[[-1, P]], channel_multiplier=1
+        )
 
-        def load_fp4_words(a):
-            w, s, g = fp4[a]
+        def load_gate_words(a):
             nc.sync.dma_start(
-                out=fw[a].bitcast(I32).rearrange("p (g c) -> p g c", g=g),
-                in_=w.bitcast(I32).rearrange("g p c -> p g c"),
+                out=gate_words[a][:, :].bitcast(I32).rearrange("p (g c) -> p g c", g=PASSES),
+                in_=[w1_words, w2_words][a].bitcast(I32).rearrange("g p c -> p g c"),
             )
 
-        def load_fp4_scales(dst, a):
-            w, s, g = fp4[a]
-            nc.sync.dma_start(
-                out=dst.bitcast(I32).rearrange("p (g c) -> p g c", g=g),
-                in_=s.bitcast(I32).rearrange("g r c -> r g c"),
-            )
-
-        def load_x_scales(eng):
-            for r in range(4):
-                eng.dma_start(
-                    out=xs_win[r:P:16, :].bitcast(I32),
-                    in_=x_scales.bitcast(I32)[:, r:16:4, :].rearrange("g q c -> q g c"),
-                )
-
-        def load_x_words(g, tag=None):
-            xw_win[g] = sb(f"xw_win{g}", [P, T], U32, tag)
+        def load_x_words(g):
             nc.sync.dma_start(
                 out=xw_win[g][:].bitcast(I32),
                 in_=x_words[g].rearrange("p n t -> p (n t)").bitcast(I32),
             )
 
-        wsrc = [w3, w4]
-        HALF = H // 2
         w_raw = {}
 
-        def load_w(a, g, lo, hi, dst):
-            rows = wsrc[a][512 * g : 512 * (g + 1), lo:hi]
-            dst = dst.rearrange("p (j c) -> p j c", j=PACK)
-            nc.sync.dma_start(out=dst, in_=rows.rearrange("(p j) c -> p j c", j=PACK))
-            return dst
-
-        fs = [fs_all[:, : 2 * N], fs_all[:, 2 * N :]]
-        s5_raw = sb("s5_raw", [P, N], U8)
-        nc.gpsimd.memset(s5_raw[:].bitcast(I32), 0)
+        def load_w(a, g, j0, j1, dst):
+            rows = [w3, w4][a][512 * g : 512 * (g + 1), :].rearrange("(p j) c -> p (j c)", j=PACK)
+            nc.sync.dma_start(out=dst, in_=rows[:, H * j0 : H * j1])
+            w_raw[(a, g, j0)] = dst.rearrange("p (j c) -> p j c", c=H)
 
         nc.sync.dma_start(lists[0][:], offs)
         nc.sync.dma_start(lists[1][:], prev)
+        nc.sync.dma_start(out=w5_raw[:].bitcast(I32), in_=w5_words[0].bitcast(I32))
         load_x_words(0)
-        load_fp4_scales(fs[0][0:16, :], 0)
-        load_fp4_scales(fs[1][0:16, :], 1)
-        load_x_scales(nc.sync)
-        for q in range(4):
-            nc.gpsimd.dma_start(
-                out=s5_raw[32 * q : 32 * q + 4, :].bitcast(I32), in_=w5_scales[0].bitcast(I32)[4 * q : 4 * q + 4, :]
+        for a in range(2):
+            nc.sync.dma_start(
+                out=gate_scales[0:16, PASSES * N * a : PASSES * N * (a + 1)].bitcast(I32).rearrange("p (g c) -> p g c", g=PASSES),
+                in_=[w1_scales, w2_scales][a].bitcast(I32).rearrange("g r c -> r g c"),
             )
-        load_x_words(1, "warm_bias")
-        fw_all = sb("fw_all", [P, 5 * 2 * N], U8, "warm_in")
-        for a in range(3):
-            fw[a] = fw_all[:, 4 * N * a : 4 * N * a + 2 * N * fp4[a][2]]
-            load_fp4_words(a)
-        first = load_w(0, 0, 0, H, sb("w_first", [P, PACK * H], F32, "warm_scale")[:])
-        for lo in (0, HALF):
-            w_raw[(0, 0, lo)] = first[:, :, lo : lo + HALF]
-
-        def deal_w5_words():
-            nc.vector.tensor_copy(
-                out=w5_dealt[:].rearrange("p (t m b) -> p t m b", t=PACK, b=2),
-                in_=fw[2].rearrange("p (m t b) -> p t m b", t=PACK, b=2),
+        nc.scalar.activation(warm_out[:], ident[:, 0:1], ACT.Sigmoid)
+        for r in range(4):
+            nc.sync.dma_start(
+                out=xs_win[r:P:16, :].bitcast(I32),
+                in_=x_scales.bitcast(I32)[:, r:16:4, :].rearrange("g q c -> q g c"),
             )
+        nc.vector.tensor_copy(
+            out=w5_dealt[:].rearrange("p (t m b) -> p t m b", t=PACK, b=2),
+            in_=w5_raw[:].rearrange("p (m t b) -> p t m b", t=PACK, b=2),
+        )
+        w_first = sb("w_first", [P, PACK * H], F32)[:, :]
+        load_w(0, 0, 0, PACK, w_first)
+        for q in range(1, 4):
+            nc.sync.dma_start(
+                out=gate_scales[32 * q : 32 * q + 4, :].bitcast(I32), in_=gate_scales[4 * q : 4 * q + 4, :].bitcast(I32)
+            )
+        load_gate_words(0)
+        load_gate_words(1)
+        load_x_words(1)
+        load_w(1, 0, 0, 2, sb("w_second", [P, 2 * H], F32)[:, :])
 
         def gather_words(a, g):
             nc.vector.tensor_copy(xw_g[a][g][:], xw_win[g][:].indirect(lists[a][:]))
 
-        w_bf = {}
-        w_codes = {}
-        w_scales = {}
+        gather_words(0, 0)
+        for a in range(2):
+            nc.vector.tensor_copy(xs_g[0][:, S * a : S * (a + 1)], xs_win[:].indirect(lists[a][:]))
+        nc.sync.dma_start(out=xs_g[1][0:112, :].bitcast(I32), in_=xs_g[0][16:128, :].bitcast(I32))
+        rest = sb("w_rest", [P, 5 * 2 * H], F32, "xs_win")
+        at = 0
+        for a, g, lo, hi in [(1, 0, 2, 4), (0, 1, 0, 4), (1, 1, 0, 4)]:
+            load_w(a, g, lo, hi, rest[:, at : at + H * (hi - lo)])
+            at = at + H * (hi - lo)
+            if (a, g, hi) == (0, 1, PACK):
+                for q in range(4):
+                    nc.sync.dma_start(
+                        out=s5_raw[32 * q : 32 * q + 4, :].bitcast(I32), in_=w5_scales[0].bitcast(I32)[4 * q : 4 * q + 4, :]
+                    )
+        gather_words(1, 0)
+        gather_words(0, 1)
+        gather_words(1, 1)
 
-        def cast_w(a, g, lo, hi, on_vector):
-            if (a, g) not in w_bf:
-                w_bf[(a, g)] = sb(f"w_bf{a}{g}", [P, PACK * H], BF16)
-            dst = w_bf[(a, g)][:, PACK * lo : PACK * hi].rearrange("p (c i j) -> p c j i", i=4, j=PACK)
-            src = w_raw[(a, g, lo)].rearrange("p j (c i) -> p c j i", i=4)
+        r_ps = [psum.tile([P, N], F32, name=f"r_ps{c}", tag=f"rbank{c}") for c in range(NCH)]
+
+        def r_pass(c, a, g):
+            nc.tensor.matmul_mx(
+                out=r_ps[c][:],
+                lhsT=xw_g[a][g][:, CH * c : CH * (c + 1)].bitcast(FP8X4),
+                lhsT_scale=xs_g[g][:, S * a + CH * c : S * a + CH * (c + 1)],
+                rhs=gate_words[a][:, 2 * N * g : 2 * N * (g + 1)].bitcast(FP4X4),
+                rhs_scale=gate_scales[:, N * (PASSES * a + g) : N * (PASSES * a + g + 1)],
+                start=(a == 0 and g == 0),
+                stop=(a == 1 and g == 1),
+            )
+
+        for a in range(2):
+            for c in range(NCH):
+                r_pass(c, a, 0)
+
+        w_bf = {(a, g): sb(f"w_bf{a}{g}", [P, PACK * H], BF16) for a in range(2) for g in range(PASSES)}
+        w_codes = {(a, g): sb(f"w_codes{a}{g}", [P, H], U32) for a in range(2) for g in range(PASSES)}
+        w_scales = {(a, g): sb(f"w_scales{a}{g}", [P, H], U8) for a in range(2) for g in range(PASSES)}
+
+        def cast_w(a, g, j0, j1, lo, hi, on_vector):
+            dst = w_bf[(a, g)][:, PACK * lo : PACK * hi].rearrange("p (c i j) -> p c j i", i=4, j=PACK)[:, :, j0:j1, :]
+            src = w_raw[(a, g, j0)][:, :, lo:hi].rearrange("p j (c i) -> p c j i", i=4)
             if on_vector:
                 nc.vector.tensor_copy(out=dst, in_=src)
             else:
                 nc.scalar.copy(out=dst, in_=src)
 
         def quantize_w(a, g, lo, hi):
-            if (a, g) not in w_codes:
-                w_codes[(a, g)] = sb(f"w_codes{a}{g}", [P, H], U32)
-                w_scales[(a, g)] = sb(f"w_scales{a}{g}", [P, H], U8)
             nc.vector.quantize_mx(
                 out=w_codes[(a, g)][:, lo:hi].bitcast(FP8X4),
                 scales=w_scales[(a, g)][:, lo:hi],
                 in_=w_bf[(a, g)][:, PACK * lo : PACK * hi],
             )
 
-        r_ps = [psum.tile([P, N], F32, name=f"r_ps{c}", tag=f"rbank{c}") for c in range(NCH)]
+        h_ps = [psum.tile([P, H], F32, name=f"h_ps{c}", tag=f"bank{c}") for c in range(NCH)]
 
-        def r_chunk(c):
-            for a, g in [(0, 0), (1, 0), (0, 1), (1, 1)]:
-                plane = xs_g if g == 0 else xs_g1
-                nc.tensor.matmul_mx(
-                    out=r_ps[c][:],
-                    lhsT=xw_g[a][g][:, CH * c : CH * (c + 1)].bitcast(FP8X4),
-                    lhsT_scale=plane[:, S * a + CH * c : S * a + CH * (c + 1)],
-                    rhs=fw[a][:, 2 * N * g : 2 * N * (g + 1)].bitcast(FP4X4),
-                    rhs_scale=fs[a][:, N * g : N * (g + 1)],
-                    start=(a == 0 and g == 0),
-                    stop=(a == 1 and g == 1),
-                )
+        def h_pass(c, a, g):
+            nc.tensor.matmul_mx(
+                out=h_ps[c][:],
+                lhsT=xw_g[a][g][:, CH * c : CH * (c + 1)].bitcast(FP8X4),
+                lhsT_scale=xs_g[g][:, S * a + CH * c : S * a + CH * (c + 1)],
+                rhs=w_codes[(a, g)][:].bitcast(FP8X4),
+                rhs_scale=w_scales[(a, g)][:],
+                start=(a == 0 and g == 0),
+                stop=(a == 1 and g == 1),
+            )
 
         sig = {}
 
         def gate(c):
-            sig_t = rest[:, PACK * H + N * c : PACK * H + N * (c + 1)].rearrange("p (t m) -> p t m", t=PACK)
+            sig_t = w_first[:, N * c : N * (c + 1)].rearrange("p (t m) -> p t m", t=PACK)
             nc.scalar.activation(sig_t, r_ps[c][:].rearrange("p (m t) -> p t m", t=PACK), ACT.Sigmoid)
             sig[c] = sig_t
 
         def turn_gate(c):
-            sig_t = sig[c]
             turned = psum.tile([P, PACK, CH], F32, name=f"turned{c}", tag=f"rbank{c}")
             for t in range(PACK):
-                nc.tensor.transpose(turned[:, t, :], sig_t[:, t, :], ident[:])
-            sig[c] = sb(f"sig{c}", [P, PACK, CH], F32)
+                nc.tensor.transpose(turned[:, t, :], sig[c][:, t, :], ident[:])
+            sig[c] = turned
+
+        def copy_gate(c, tag=None):
+            turned = sig[c]
+            sig[c] = sb(f"sig{c}", [P, PACK, CH], F32, tag)
             nc.scalar.copy(sig[c][:], turned[:])
 
-        gather_words(0, 0)
-        for q in range(1, 4):
-            nc.scalar.dma_start(
-                out=fs_all[32 * q : 32 * q + 4, :].bitcast(I32), in_=fs_all[4 * q : 4 * q + 4, :].bitcast(I32)
-            )
-        for a in range(2):
-            nc.vector.tensor_copy(xs_g[:, S * a : S * (a + 1)], xs_win[:].indirect(lists[a][:]))
-        nc.sync.dma_start(out=xs_g1[0:112, :].bitcast(I32), in_=xs_g[16:128, :].bitcast(I32))
-        rest = sb("w_rest", [P, 3 * PACK * H], F32, "xs_win")
-        pieces = [(1, 0, 0, 256), (1, 0, 256, 512), (0, 1, 0, 256), (0, 1, 256, 512), (1, 1, 0, 256), (1, 1, 256, 384), (1, 1, 384, 512)]
-        at = 0
-        for a, g, lo, hi in pieces:
-            w_raw[(a, g, lo)] = load_w(a, g, lo, hi, rest[:, at : at + PACK * (hi - lo)])
-            at = at + PACK * (hi - lo)
-        gather_words(1, 0)
-        gather_words(0, 1)
-        gather_words(1, 1)
-        for c in range(NCH):
-            r_chunk(c)
-        deal_w5_words()
-        s5_dealt = sb("s5_dealt", [P, N], U8, "xw_win1")
-        nc.vector.tensor_copy(
-            out=s5_dealt[:].rearrange("p (t m) -> p t m", t=PACK), in_=s5_raw[:].rearrange("p (m t) -> p t m", t=PACK)
-        )
-        cast_w(0, 0, 0, 256, False)
-        cast_w(0, 0, 256, 512, True)
+        cast_w(0, 0, 0, PACK, 0, H, False)
+        cast_w(1, 0, 0, 2, 0, H, False)
         quantize_w(0, 0, 0, H)
-        cast_w(1, 0, 0, 256, False)
-        cast_w(1, 0, 256, 512, True)
-        quantize_w(1, 0, 0, H)
-        cast_w(0, 1, 0, 256, False)
-        cast_w(0, 1, 256, 512, True)
-        quantize_w(0, 1, 0, H)
-        cast_w(1, 1, 0, 256, True)
-        cast_w(1, 1, 256, 384, True)
-        quantize_w(1, 1, 0, 256)
-        cast_w(1, 1, 384, 512, True)
-        quantize_w(1, 1, 256, 384)
-        quantize_w(1, 1, 384, 512)
+        for c in range(NCH):
+            h_pass(c, 0, 0)
+        for c in range(NCH):
+            for a in range(2):
+                r_pass(c, a, 1)
         for c in range(NCH):
             gate(c)
         for c in range(NCH):
             turn_gate(c)
+        for c in range(NCH - 1):
+            copy_gate(c)
+        cast_w(1, 0, 2, PACK, 0, H, True)
+        quantize_w(1, 0, 0, H)
+        for c in range(NCH):
+            h_pass(c, 1, 0)
+        cast_w(0, 1, 0, PACK, 0, H, True)
+        quantize_w(0, 1, 0, H)
+        for c in range(NCH):
+            h_pass(c, 0, 1)
+        cast_w(1, 1, 0, PACK, 0, 256, True)
+        cast_w(1, 1, 0, PACK, 256, 384, True)
+        cast_w(1, 1, 0, PACK, 384, H, False)
+        copy_gate(NCH - 1, "xs_win")
+        quantize_w(1, 1, 0, 256)
+        quantize_w(1, 1, 256, H)
+        for c in range(NCH):
+            h_pass(c, 1, 1)
+        s5_dealt = sb("s5_dealt", [P, N], U8, "w_bf11")
+        nc.vector.tensor_copy(
+            out=s5_dealt[:].rearrange("p (t m) -> p t m", t=PACK), in_=s5_raw[:].rearrange("p (m t) -> p t m", t=PACK)
+        )
+
 
         o_codes = sb("o_codes", [P, S], U32)
         o_scales = sb("o_scales", [P, S], U8)
         out_v = out_0.rearrange("(p t) n -> p t n", t=PACK)
-        order = [(0, 0), (1, 0), (0, 1), (1, 1)]
         st = {}
 
-        def h_mm(c):
-            h_ps = psum.tile([P, H], F32, name=f"h_ps{c}", tag=f"bank{c}")
-            for i, (a, g) in enumerate(order):
-                nc.tensor.matmul_mx(
-                    out=h_ps[:],
-                    lhsT=xw_g[a][g][:, CH * c : CH * (c + 1)].bitcast(FP8X4),
-                    lhsT_scale=(xs_g if g == 0 else xs_g1)[:, S * a + CH * c : S * a + CH * (c + 1)],
-                    rhs=w_codes[(a, g)][:].bitcast(FP8X4),
-                    rhs_scale=w_scales[(a, g)][:],
-                    start=(i == 0),
-                    stop=(i == 3),
-                )
-            st[("h", c)] = h_ps
-
-        def h_quant(c):
+        def relu_h(c, on_vector):
             h_t = sb(f"h_t{c}", [P, H], BF16)
-            nc.scalar.activation(
-                h_t[:].rearrange("p (u m e) -> p u m e", u=2, e=2),
-                st[("h", c)][:].rearrange("p (m u e) -> p u m e", u=2, e=2),
-                ACT.Relu,
-            )
+            dst = h_t[:].rearrange("p (u m e) -> p u m e", u=2, e=2)
+            src = h_ps[c][:].rearrange("p (m u e) -> p u m e", u=2, e=2)
+            if on_vector:
+                nc.vector.tensor_scalar(dst, src, 0.0, None, ALU.max)
+            else:
+                nc.scalar.activation(dst, src, ACT.Relu)
+            st[("ht", c)] = h_t
+
+        def turn_h(c):
             pairs = psum.tile([P, 2, CH], F32, name=f"pairs{c}", tag=f"bank{c}")
             for u in range(2):
-                nc.tensor.transpose(pairs[:, u, :], h_t[:].bitcast(F32)[:, P * u : P * (u + 1)], ident[:])
+                nc.tensor.transpose(pairs[:, u, :], st[("ht", c)][:].bitcast(F32)[:, P * u : P * (u + 1)], ident[:])
+            st[("pairs", c)] = pairs
+
+        def weave_h(c, on_vector):
             h_bf = sb(f"h_bf{c}", [P, CH * PACK], BF16)
-            nc.vector.tensor_copy(
-                out=h_bf[:].bitcast(F32).rearrange("p (n u) -> p n u", u=2), in_=pairs[:].rearrange("p u n -> p n u")
-            )
+            dst = h_bf[:].bitcast(F32).rearrange("p (n u) -> p n u", u=2)
+            src = st[("pairs", c)][:].rearrange("p u n -> p n u")
+            if on_vector:
+                nc.vector.tensor_copy(out=dst, in_=src)
+            else:
+                nc.scalar.copy(out=dst, in_=src)
+            st[("hbf", c)] = h_bf
+
+        def quant_h(c):
             h_codes = sb(f"h_codes{c}", [P, CH], U32)
             h_scales = sb(f"h_scales{c}", [P, CH], U8)
-            nc.vector.quantize_mx(out=h_codes[:].bitcast(FP8X4), scales=h_scales[:], in_=h_bf[:])
+            nc.vector.quantize_mx(out=h_codes[:].bitcast(FP8X4), scales=h_scales[:], in_=st[("hbf", c)][:])
             st[("hq", c)] = (h_codes, h_scales)
 
         def y_mm(c):
@@ -290,32 +296,39 @@ def tile_picked_zshift_relu_po_kernel(
             nc.sync.dma_start(out=out_v[:, :, cols], in_=o[:])
             st[("o", c)] = o
 
+        o_bf = sb("o_bf", [P, S * PACK], BF16)
+
         def cast_o(c):
-            o_bf = sb(f"o_bf{c}", [P, CH * PACK], BF16)
             nc.scalar.copy(
-                out=o_bf[:].rearrange("p (c i t) -> p c t i", i=4, t=PACK),
+                out=o_bf[:, PACK * CH * c : PACK * CH * (c + 1)].rearrange("p (c i t) -> p c t i", i=4, t=PACK),
                 in_=st[("o", c)][:].rearrange("p t (c i) -> p c t i", i=4),
             )
-            st[("obf", c)] = o_bf
 
-        def quant_o(c):
-            cols = slice(CH * c, CH * (c + 1))
-            nc.vector.quantize_mx(out=o_codes[:, cols].bitcast(FP8X4), scales=o_scales[:, cols], in_=st[("obf", c)][:])
+        def quant_o(lo, hi):
+            cols = slice(CH * lo, CH * hi)
+            nc.vector.quantize_mx(
+                out=o_codes[:, cols].bitcast(FP8X4), scales=o_scales[:, cols], in_=o_bf[:, PACK * CH * lo : PACK * CH * hi]
+            )
             nc.sync.dma_start(
                 out=out_1[0].rearrange("p n t -> p (n t)").bitcast(I32)[:, cols], in_=o_codes[:, cols].bitcast(I32)
             )
 
         for c in range(NCH):
-            h_mm(c)
-        for step in range(NCH + 2):
-            if step < NCH:
-                h_quant(step)
-                y_mm(step)
-            if 1 <= step < NCH + 1:
-                finish(step - 1)
-                cast_o(step - 1)
-            if 2 <= step:
-                quant_o(step - 2)
+            relu_h(c, c == 1)
+        for c in range(NCH):
+            turn_h(c)
+        for c in range(NCH):
+            weave_h(c, c < 2)
+        for c in range(NCH):
+            quant_h(c)
+        for c in range(NCH):
+            y_mm(c)
+        for c in range(NCH):
+            finish(c)
+            cast_o(c)
+        quant_o(0, 2)
+        quant_o(2, 3)
+        quant_o(3, 4)
         for q in range(4):
             eng = nc.scalar if q % 2 else nc.sync
             eng.dma_start(

@@ -42,37 +42,41 @@ def tile_picked_zshift_relu_po_kernel(
         lists = [keep.tile([P, S // 16], U16, name="offs_sb"), keep.tile([P, S // 16], U16, name="prev_sb")]
         xs_win = sb("xs_win", [P, T], U8)
         ones = sb("ones", [P, P], F32)
-        xw_win = [sb("xw_win0", [P, T], U32), placed("xw_win1", [P, T], U32, 4 * T + 8 * N + N)]
-        W5_AT = 4 * T + 8 * N
-        w5_raw = placed("w5_raw", [P, 2 * N], U8, W5_AT)
+        xw_win = [sb(f"xw_win{g}", [P, T], U32)[:, :] for g in range(PASSES)]
+        w5_raw = sb("w5_raw", [P, 2 * N], U8)[:, :]
+        gate_words = [sb(f"gate_words{a}", [P, PASSES * 2 * N], U8)[:, :] for a in range(2)]
         xs_g = [sb(f"xs_g{g}", [P, 2 * S], U8) for g in range(PASSES)]
         xw_g = [[sb(f"xw_g{a}{g}", [P, S], U32) for g in range(PASSES)] for a in range(2)]
-        gate_words_all = placed("gate_words", [P, 2 * PASSES * 2 * N], U8, W5_AT + N - 8 * N)
-        gate_words = [gate_words_all[:, PASSES * 2 * N * a : PASSES * 2 * N * (a + 1)] for a in range(2)]
-        gate_scales = sb("gate_scales", [P, 2 * PASSES * N], U8)
-        s5_raw = sb("s5_raw", [P, N], U8)
+        gate_scales = [sb(f"gate_scales{a}", [P, PASSES * N], U8) for a in range(2)]
         w5_dealt = sb("w5_dealt", [P, 2 * N], U8)
         ident = sb("ident", [P, P], F32)
         warm_out = sb("warm_out", [P, 1], F32)
 
-        nc.vector.memset(gate_scales[:].bitcast(I32), 0)
-        nc.vector.memset(xs_g[1][:].bitcast(I32), 0)
-        nc.vector.memset(s5_raw[:].bitcast(I32), 0)
         nc.gpsimd.memset(xs_win[:].bitcast(I32), 0)
         nc.gpsimd.memset(ones[:], 1.0)
         nc.gpsimd.affine_select(
             out=ident[:], in_=ones[:], compare_op=ALU.is_equal, fill=0.0, base=0, pattern=[[-1, P]], channel_multiplier=1
         )
+        for a in range(2):
+            nc.vector.memset(gate_scales[a][:].bitcast(I32), 0)
+        nc.vector.memset(xs_g[1][:].bitcast(I32), 0)
 
         def load_gate_words(a):
             nc.sync.dma_start(
-                out=gate_words[a][:, :].bitcast(I32).rearrange("p (g c) -> p g c", g=PASSES),
+                out=gate_words[a].bitcast(I32).rearrange("p (g c) -> p g c", g=PASSES),
                 in_=[w1_words, w2_words][a].bitcast(I32).rearrange("g p c -> p g c"),
             )
 
+        def load_gate_scales(a):
+            for q in range(4):
+                nc.sync.dma_start(
+                    out=gate_scales[a][32 * q : 32 * q + 4, :].bitcast(I32).rearrange("p (g c) -> p g c", g=PASSES),
+                    in_=[w1_scales, w2_scales][a].bitcast(I32)[:, 4 * q : 4 * q + 4, :].rearrange("g r c -> r g c"),
+                )
+
         def load_x_words(g):
             nc.sync.dma_start(
-                out=xw_win[g][:].bitcast(I32),
+                out=xw_win[g].bitcast(I32),
                 in_=x_words[g].rearrange("p n t -> p (n t)").bitcast(I32),
             )
 
@@ -83,54 +87,49 @@ def tile_picked_zshift_relu_po_kernel(
             nc.sync.dma_start(out=dst, in_=rows[:, H * j0 : H * j1])
             w_raw[(a, g, j0)] = dst.rearrange("p (j c) -> p j c", c=H)
 
+        def gather_words(a, g, lo=0, hi=S):
+            nc.vector.tensor_copy(xw_g[a][g][:, lo:hi], xw_win[g].indirect(lists[a][:, lo // 16 : hi // 16]))
+
         nc.sync.dma_start(lists[0][:], offs)
         nc.sync.dma_start(lists[1][:], prev)
-        nc.sync.dma_start(out=w5_raw[:].bitcast(I32), in_=w5_words[0].bitcast(I32))
-        load_x_words(0)
-        for a in range(2):
-            nc.sync.dma_start(
-                out=gate_scales[0:16, PASSES * N * a : PASSES * N * (a + 1)].bitcast(I32).rearrange("p (g c) -> p g c", g=PASSES),
-                in_=[w1_scales, w2_scales][a].bitcast(I32).rearrange("g r c -> r g c"),
-            )
+        load_gate_words(0)
         nc.scalar.activation(warm_out[:], ident[:, 0:1], ACT.Sigmoid)
         for r in range(4):
             nc.sync.dma_start(
                 out=xs_win[r:P:16, :].bitcast(I32),
                 in_=x_scales.bitcast(I32)[:, r:16:4, :].rearrange("g q c -> q g c"),
             )
-        nc.vector.tensor_copy(
-            out=w5_dealt[:].rearrange("p (t m b) -> p t m b", t=PACK, b=2),
-            in_=w5_raw[:].rearrange("p (m t b) -> p t m b", t=PACK, b=2),
-        )
-        w_first = sb("w_first", [P, PACK * H], F32)[:, :]
-        load_w(0, 0, 0, PACK, w_first)
-        for q in range(1, 4):
-            nc.sync.dma_start(
-                out=gate_scales[32 * q : 32 * q + 4, :].bitcast(I32), in_=gate_scales[4 * q : 4 * q + 4, :].bitcast(I32)
-            )
-        load_gate_words(0)
+        load_x_words(0)
         load_gate_words(1)
+        load_gate_scales(0)
+        nc.sync.dma_start(out=w5_raw.bitcast(I32), in_=w5_words[0].bitcast(I32))
         load_x_words(1)
-        load_w(1, 0, 0, 2, sb("w_second", [P, 2 * H], F32)[:, :])
-
-        def gather_words(a, g):
-            nc.vector.tensor_copy(xw_g[a][g][:], xw_win[g][:].indirect(lists[a][:]))
-
-        gather_words(0, 0)
         for a in range(2):
             nc.vector.tensor_copy(xs_g[0][:, S * a : S * (a + 1)], xs_win[:].indirect(lists[a][:]))
         nc.sync.dma_start(out=xs_g[1][0:112, :].bitcast(I32), in_=xs_g[0][16:128, :].bitcast(I32))
-        rest = sb("w_rest", [P, 5 * 2 * H], F32, "xs_win")
-        at = 0
-        for a, g, lo, hi in [(1, 0, 2, 4), (0, 1, 0, 4), (1, 1, 0, 4)]:
-            load_w(a, g, lo, hi, rest[:, at : at + H * (hi - lo)])
-            at = at + H * (hi - lo)
-            if (a, g, hi) == (0, 1, PACK):
-                for q in range(4):
-                    nc.sync.dma_start(
-                        out=s5_raw[32 * q : 32 * q + 4, :].bitcast(I32), in_=w5_scales[0].bitcast(I32)[4 * q : 4 * q + 4, :]
-                    )
+        load_gate_scales(1)
+        raw_early = sb("raw_early", [P, 2 * PACK * H], F32, "xs_win")
+        load_w(0, 0, 0, 2, raw_early[:, : 2 * H])
+        load_w(0, 0, 2, PACK, raw_early[:, 2 * H : PACK * H])
+        load_w(1, 0, 0, PACK, raw_early[:, PACK * H :])
+        sig_late = sb("sig_late", [P, 2 * N], F32)
+        sig_rows = [raw_early[:, :N], raw_early[:, N : 2 * N], sig_late[:, :N], sig_late[:, N:]]
+        nc.vector.tensor_copy(
+            out=w5_dealt[:].rearrange("p (t m b) -> p t m b", t=PACK, b=2),
+            in_=w5_raw.rearrange("p (m t b) -> p t m b", t=PACK, b=2),
+        )
+        s5_raw = sb("s5_raw", [P, N], U8, "w5_raw")
+        nc.vector.memset(s5_raw[:].bitcast(I32), 0)
+        for q in range(4):
+            nc.sync.dma_start(
+                out=s5_raw[32 * q : 32 * q + 4, :].bitcast(I32), in_=w5_scales[0].bitcast(I32)[4 * q : 4 * q + 4, :]
+            )
+        gather_words(0, 0, 0, S // 2)
+        gather_words(0, 0, S // 2, S)
         gather_words(1, 0)
+        raw_late = sb("raw_late", [P, 2 * PACK * H], F32, "xw_win0")
+        load_w(0, 1, 0, PACK, raw_late[:, : PACK * H])
+        load_w(1, 1, 0, PACK, raw_late[:, PACK * H :])
         gather_words(0, 1)
         gather_words(1, 1)
 
@@ -142,7 +141,7 @@ def tile_picked_zshift_relu_po_kernel(
                 lhsT=xw_g[a][g][:, CH * c : CH * (c + 1)].bitcast(FP8X4),
                 lhsT_scale=xs_g[g][:, S * a + CH * c : S * a + CH * (c + 1)],
                 rhs=gate_words[a][:, 2 * N * g : 2 * N * (g + 1)].bitcast(FP4X4),
-                rhs_scale=gate_scales[:, N * (PASSES * a + g) : N * (PASSES * a + g + 1)],
+                rhs_scale=gate_scales[a][:, N * g : N * (g + 1)],
                 start=(a == 0 and g == 0),
                 stop=(a == 1 and g == 1),
             )
@@ -156,8 +155,8 @@ def tile_picked_zshift_relu_po_kernel(
         w_scales = {(a, g): sb(f"w_scales{a}{g}", [P, H], U8) for a in range(2) for g in range(PASSES)}
 
         def cast_w(a, g, j0, j1, lo, hi, on_vector):
-            dst = w_bf[(a, g)][:, PACK * lo : PACK * hi].rearrange("p (c i j) -> p c j i", i=4, j=PACK)[:, :, j0:j1, :]
-            src = w_raw[(a, g, j0)][:, :, lo:hi].rearrange("p j (c i) -> p c j i", i=4)
+            dst = w_bf[(a, g)][:].rearrange("p (t m j) -> p m j t", t=PACK, j=PACK)[:, lo // PACK : hi // PACK, j0:j1, :]
+            src = w_raw[(a, g, j0)][:, :, lo:hi].rearrange("p j (m t) -> p m j t", t=PACK)
             if on_vector:
                 nc.vector.tensor_copy(out=dst, in_=src)
             else:
@@ -170,23 +169,24 @@ def tile_picked_zshift_relu_po_kernel(
                 in_=w_bf[(a, g)][:, PACK * lo : PACK * hi],
             )
 
-        h_ps = [psum.tile([P, H], F32, name=f"h_ps{c}", tag=f"bank{c}") for c in range(NCH)]
+        h_ps = [psum.tile([P, PACK, CH], F32, name=f"h_ps{c}", tag=f"bank{c}") for c in range(NCH)]
 
         def h_pass(c, a, g):
-            nc.tensor.matmul_mx(
-                out=h_ps[c][:],
-                lhsT=xw_g[a][g][:, CH * c : CH * (c + 1)].bitcast(FP8X4),
-                lhsT_scale=xs_g[g][:, S * a + CH * c : S * a + CH * (c + 1)],
-                rhs=w_codes[(a, g)][:].bitcast(FP8X4),
-                rhs_scale=w_scales[(a, g)][:],
-                start=(a == 0 and g == 0),
-                stop=(a == 1 and g == 1),
-            )
+            for t in range(PACK):
+                nc.tensor.matmul_mx(
+                    out=h_ps[c][:, t, :],
+                    lhsT=w_codes[(a, g)][:, P * t : P * (t + 1)].bitcast(FP8X4),
+                    lhsT_scale=w_scales[(a, g)][:, P * t : P * (t + 1)],
+                    rhs=xw_g[a][g][:, CH * c : CH * (c + 1)].bitcast(FP8X4),
+                    rhs_scale=xs_g[g][:, S * a + CH * c : S * a + CH * (c + 1)],
+                    start=(a == 0 and g == 0 and t == 0),
+                    stop=(a == 1 and g == 1 and t == PACK - 1),
+                )
 
         sig = {}
 
         def gate(c):
-            sig_t = w_first[:, N * c : N * (c + 1)].rearrange("p (t m) -> p t m", t=PACK)
+            sig_t = sig_rows[c].rearrange("p (t m) -> p t m", t=PACK)
             nc.scalar.activation(sig_t, r_ps[c][:].rearrange("p (m t) -> p t m", t=PACK), ACT.Sigmoid)
             sig[c] = sig_t
 
@@ -196,26 +196,26 @@ def tile_picked_zshift_relu_po_kernel(
                 nc.tensor.transpose(turned[:, t, :], sig[c][:, t, :], ident[:])
             sig[c] = turned
 
-        def copy_gate(c, tag=None):
+        def copy_gate(c, dst):
             turned = sig[c]
-            sig[c] = sb(f"sig{c}", [P, PACK, CH], F32, tag)
-            nc.scalar.copy(sig[c][:], turned[:])
+            sig[c] = dst.rearrange("p (t n) -> p t n", t=PACK)
+            nc.scalar.copy(sig[c], turned[:])
 
-        cast_w(0, 0, 0, PACK, 0, H, False)
-        cast_w(1, 0, 0, 2, 0, H, False)
+        for c in range(NCH):
+            r_pass(c, 0, 1)
+        for c in range(NCH):
+            r_pass(c, 1, 1)
+        cast_w(0, 0, 0, 2, 0, H, False)
+        cast_w(0, 0, 2, PACK, 0, H, True)
         quantize_w(0, 0, 0, H)
-        for c in range(NCH):
-            h_pass(c, 0, 0)
-        for c in range(NCH):
-            for a in range(2):
-                r_pass(c, a, 1)
         for c in range(NCH):
             gate(c)
         for c in range(NCH):
             turn_gate(c)
+            h_pass(c, 0, 0)
         for c in range(NCH - 1):
-            copy_gate(c)
-        cast_w(1, 0, 2, PACK, 0, H, True)
+            copy_gate(c, sb(f"sig{c}", [P, N], F32)[:, :])
+        cast_w(1, 0, 0, PACK, 0, H, True)
         quantize_w(1, 0, 0, H)
         for c in range(NCH):
             h_pass(c, 1, 0)
@@ -223,15 +223,14 @@ def tile_picked_zshift_relu_po_kernel(
         quantize_w(0, 1, 0, H)
         for c in range(NCH):
             h_pass(c, 0, 1)
-        cast_w(1, 1, 0, PACK, 0, 256, True)
-        cast_w(1, 1, 0, PACK, 256, 384, True)
-        cast_w(1, 1, 0, PACK, 384, H, False)
-        copy_gate(NCH - 1, "xs_win")
+        cast_w(1, 1, 0, PACK, 0, 320, True)
+        cast_w(1, 1, 0, PACK, 320, H, False)
+        copy_gate(NCH - 1, raw_late[:, PACK * H : PACK * H + N])
         quantize_w(1, 1, 0, 256)
         quantize_w(1, 1, 256, H)
         for c in range(NCH):
             h_pass(c, 1, 1)
-        s5_dealt = sb("s5_dealt", [P, N], U8, "w_bf11")
+        s5_dealt = sb("s5_dealt", [P, N], U8)
         nc.vector.tensor_copy(
             out=s5_dealt[:].rearrange("p (t m) -> p t m", t=PACK), in_=s5_raw[:].rearrange("p (m t) -> p t m", t=PACK)
         )
@@ -243,29 +242,13 @@ def tile_picked_zshift_relu_po_kernel(
         st = {}
 
         def relu_h(c, on_vector):
-            h_t = sb(f"h_t{c}", [P, H], BF16)
-            dst = h_t[:].rearrange("p (u m e) -> p u m e", u=2, e=2)
-            src = h_ps[c][:].rearrange("p (m u e) -> p u m e", u=2, e=2)
+            h_bf = sb(f"h_bf{c}", [P, CH * PACK], BF16)
+            dst = h_bf[:].rearrange("p (n t) -> p n t", t=PACK)
+            src = h_ps[c][:].rearrange("p t n -> p n t")
             if on_vector:
                 nc.vector.tensor_scalar(dst, src, 0.0, None, ALU.max)
             else:
                 nc.scalar.activation(dst, src, ACT.Relu)
-            st[("ht", c)] = h_t
-
-        def turn_h(c):
-            pairs = psum.tile([P, 2, CH], F32, name=f"pairs{c}", tag=f"bank{c}")
-            for u in range(2):
-                nc.tensor.transpose(pairs[:, u, :], st[("ht", c)][:].bitcast(F32)[:, P * u : P * (u + 1)], ident[:])
-            st[("pairs", c)] = pairs
-
-        def weave_h(c, on_vector):
-            h_bf = sb(f"h_bf{c}", [P, CH * PACK], BF16)
-            dst = h_bf[:].bitcast(F32).rearrange("p (n u) -> p n u", u=2)
-            src = st[("pairs", c)][:].rearrange("p u n -> p n u")
-            if on_vector:
-                nc.vector.tensor_copy(out=dst, in_=src)
-            else:
-                nc.scalar.copy(out=dst, in_=src)
             st[("hbf", c)] = h_bf
 
         def quant_h(c):
@@ -276,7 +259,7 @@ def tile_picked_zshift_relu_po_kernel(
 
         def y_mm(c):
             h_codes, h_scales = st[("hq", c)]
-            y_ps = psum.tile([P, PACK, CH], F32, name=f"y_ps{c}", tag=f"bank{c}")
+            y_ps = psum.tile([P, PACK, CH], F32, name=f"y_ps{c}", tag=f"rbank{c}")
             for t in range(PACK):
                 nc.tensor.matmul_mx(
                     out=y_ps[:, t, :],
@@ -292,7 +275,7 @@ def tile_picked_zshift_relu_po_kernel(
         def finish(c):
             cols = slice(CH * c, CH * (c + 1))
             o = sb(f"o{c}", [P, PACK, CH], F32)
-            nc.vector.tensor_tensor(o[:], st[("y", c)][:], sig[c][:], ALU.mult)
+            nc.vector.tensor_tensor(o[:], st[("y", c)][:], sig[c], ALU.mult)
             nc.sync.dma_start(out=out_v[:, :, cols], in_=o[:])
             st[("o", c)] = o
 
@@ -315,10 +298,6 @@ def tile_picked_zshift_relu_po_kernel(
 
         for c in range(NCH):
             relu_h(c, c == 1)
-        for c in range(NCH):
-            turn_h(c)
-        for c in range(NCH):
-            weave_h(c, c < 2)
         for c in range(NCH):
             quant_h(c)
         for c in range(NCH):

@@ -68,10 +68,10 @@ def tile_picked_zshift_relu_po_kernel(
             )
 
         def load_gate_scales(a):
-            for q in range(4):
+            for r in range(4):
                 nc.sync.dma_start(
-                    out=gate_scales[a][32 * q : 32 * q + 4, :].bitcast(I32).rearrange("p (g c) -> p g c", g=PASSES),
-                    in_=[w1_scales, w2_scales][a].bitcast(I32)[:, 4 * q : 4 * q + 4, :].rearrange("g r c -> r g c"),
+                    out=gate_scales[a][r:P:32, :].bitcast(I32).rearrange("p (g c) -> p g c", g=PASSES),
+                    in_=[w1_scales, w2_scales][a].bitcast(I32)[:, r:16:4, :].rearrange("g q c -> q g c"),
                 )
 
         def load_x_words(g):
@@ -120,10 +120,8 @@ def tile_picked_zshift_relu_po_kernel(
         )
         s5_raw = sb("s5_raw", [P, N], U8, "w5_raw")
         nc.vector.memset(s5_raw[:].bitcast(I32), 0)
-        for q in range(4):
-            nc.sync.dma_start(
-                out=s5_raw[32 * q : 32 * q + 4, :].bitcast(I32), in_=w5_scales[0].bitcast(I32)[4 * q : 4 * q + 4, :]
-            )
+        for r in range(4):
+            nc.sync.dma_start(out=s5_raw[r:P:32, :].bitcast(I32), in_=w5_scales[0].bitcast(I32)[r:16:4, :])
         gather_words(0, 0, 0, S // 2)
         gather_words(0, 0, S // 2, S)
         gather_words(1, 0)

@@ -31,18 +31,18 @@ def tile_picked_zshift_relu_po_kernel(
         keep = ctx.enter_context(tc.tile_pool(name="keep", bufs=1))
         psum = ctx.enter_context(tc.psum_pool(name="psum", bufs=1))
 
-        shared = ctx.enter_context(tc.tile_pool(name="shared", bufs=1))
+        late = ctx.enter_context(tc.tile_pool(name="late", bufs=1))
+
+        def placed(name, shape, dtype, offset):
+            return late.tile(shape, dtype, name=name, align_bytes=64, offset=offset)
 
         def sb(name, shape, dtype, tag=None):
             return keep.tile(shape, dtype, name=name, tag=tag or name, align_bytes=64)
 
-        def placed(name, shape, dtype, offset):
-            return shared.tile(shape, dtype, name=name, align_bytes=64, offset=offset)
-
         lists = [keep.tile([P, S // 16], U16, name="offs_sb"), keep.tile([P, S // 16], U16, name="prev_sb")]
         xs_win = sb("xs_win", [P, T], U8)
         ones = sb("ones", [P, P], F32)
-        xw_win = [sb(f"xw_win{g}", [P, T], U32)[:, :] for g in range(PASSES)]
+        xw_win = [placed("xw_win0", [P, 2 * T + N // 4], U32, 0)[:, :T], sb("xw_win1", [P, T], U32)[:, :]]
         w5_raw = sb("w5_raw", [P, 2 * N], U8)[:, :]
         gate_words = [sb(f"gate_words{a}", [P, PASSES * 2 * N], U8)[:, :] for a in range(2)]
         xs_g = [sb(f"xs_g{g}", [P, 2 * S], U8) for g in range(PASSES)]
@@ -102,34 +102,31 @@ def tile_picked_zshift_relu_po_kernel(
         load_x_words(0)
         load_gate_words(1)
         load_gate_scales(0)
-        nc.sync.dma_start(out=w5_raw.bitcast(I32), in_=w5_words[0].bitcast(I32))
         load_x_words(1)
+        nc.sync.dma_start(out=w5_raw.bitcast(I32), in_=w5_words[0].bitcast(I32))
+        load_gate_scales(1)
         for a in range(2):
             nc.vector.tensor_copy(xs_g[0][:, S * a : S * (a + 1)], xs_win[:].indirect(lists[a][:]))
         nc.sync.dma_start(out=xs_g[1][0:112, :].bitcast(I32), in_=xs_g[0][16:128, :].bitcast(I32))
-        load_gate_scales(1)
         raw_early = sb("raw_early", [P, 2 * PACK * H], F32, "xs_win")
-        load_w(0, 0, 0, 2, raw_early[:, : 2 * H])
-        load_w(0, 0, 2, PACK, raw_early[:, 2 * H : PACK * H])
+        load_w(0, 0, 0, PACK, raw_early[:, : PACK * H])
         load_w(1, 0, 0, PACK, raw_early[:, PACK * H :])
-        sig_late = sb("sig_late", [P, 2 * N], F32)
-        sig_rows = [raw_early[:, :N], raw_early[:, N : 2 * N], sig_late[:, :N], sig_late[:, N:]]
-        nc.vector.tensor_copy(
-            out=w5_dealt[:].rearrange("p (t m b) -> p t m b", t=PACK, b=2),
-            in_=w5_raw.rearrange("p (m t b) -> p t m b", t=PACK, b=2),
-        )
-        s5_raw = sb("s5_raw", [P, N], U8, "w5_raw")
-        nc.vector.memset(s5_raw[:].bitcast(I32), 0)
-        for r in range(4):
-            nc.sync.dma_start(out=s5_raw[r:P:32, :].bitcast(I32), in_=w5_scales[0].bitcast(I32)[r:16:4, :])
         gather_words(0, 0, 0, S // 2)
         gather_words(0, 0, S // 2, S)
         gather_words(1, 0)
-        raw_late = sb("raw_late", [P, 2 * PACK * H], F32, "xw_win0")
+        raw_late = placed("raw_late", [P, 2 * PACK * H], F32, 0)
+        s5_raw = placed("s5_raw", [P, N], U8, 8 * T)
+        nc.vector.memset(s5_raw[:].bitcast(I32), 0)
         load_w(0, 1, 0, PACK, raw_late[:, : PACK * H])
+        for r in range(4):
+            nc.sync.dma_start(out=s5_raw[r:P:32, :].bitcast(I32), in_=w5_scales[0].bitcast(I32)[r:16:4, :])
         load_w(1, 1, 0, PACK, raw_late[:, PACK * H :])
         gather_words(0, 1)
         gather_words(1, 1)
+        nc.vector.tensor_copy(
+            out=w5_dealt[:].bitcast(U16).rearrange("p (t m) -> p t m", t=PACK),
+            in_=w5_raw.bitcast(U16).rearrange("p (m t) -> p t m", t=PACK),
+        )
 
         r_ps = [psum.tile([P, N], F32, name=f"r_ps{c}", tag=f"rbank{c}") for c in range(NCH)]
 
@@ -184,7 +181,7 @@ def tile_picked_zshift_relu_po_kernel(
         sig = {}
 
         def gate(c):
-            sig_t = sig_rows[c].rearrange("p (t m) -> p t m", t=PACK)
+            sig_t = sb(f"sig_rows{c}", [P, PACK, P], F32)[:]
             nc.scalar.activation(sig_t, r_ps[c][:].rearrange("p (m t) -> p t m", t=PACK), ACT.Sigmoid)
             sig[c] = sig_t
 
@@ -196,34 +193,37 @@ def tile_picked_zshift_relu_po_kernel(
 
         def copy_gate(c, dst):
             turned = sig[c]
-            sig[c] = dst.rearrange("p (t n) -> p t n", t=PACK)
+            sig[c] = dst
             nc.scalar.copy(sig[c], turned[:])
 
         for c in range(NCH):
             r_pass(c, 0, 1)
         for c in range(NCH):
             r_pass(c, 1, 1)
-        cast_w(0, 0, 0, 2, 0, H, False)
-        cast_w(0, 0, 2, PACK, 0, H, True)
+        cast_w(0, 0, 0, PACK, 0, H, True)
         quantize_w(0, 0, 0, H)
         for c in range(NCH):
             gate(c)
-        for c in range(NCH):
+        for c in range(NCH // 2):
             turn_gate(c)
+        for c in range(NCH):
             h_pass(c, 0, 0)
+        for c in range(NCH // 2, NCH):
+            turn_gate(c)
         for c in range(NCH - 1):
-            copy_gate(c, sb(f"sig{c}", [P, N], F32)[:, :])
+            copy_gate(c, sb(f"sig{c}", [P, PACK, CH], F32)[:])
         cast_w(1, 0, 0, PACK, 0, H, True)
         quantize_w(1, 0, 0, H)
         for c in range(NCH):
             h_pass(c, 1, 0)
-        cast_w(0, 1, 0, PACK, 0, H, True)
+        cast_w(0, 1, 0, PACK, 0, 384, True)
+        cast_w(0, 1, 0, PACK, 384, H, False)
         quantize_w(0, 1, 0, H)
         for c in range(NCH):
             h_pass(c, 0, 1)
         cast_w(1, 1, 0, PACK, 0, 320, True)
         cast_w(1, 1, 0, PACK, 320, H, False)
-        copy_gate(NCH - 1, raw_late[:, PACK * H : PACK * H + N])
+        copy_gate(NCH - 1, w_raw[(1, 1, 0)][:, :, H - CH :])
         quantize_w(1, 1, 0, 256)
         quantize_w(1, 1, 256, H)
         for c in range(NCH):
@@ -285,14 +285,19 @@ def tile_picked_zshift_relu_po_kernel(
                 in_=st[("o", c)][:].rearrange("p t (c i) -> p c t i", i=4),
             )
 
-        def quant_o(lo, hi):
+        def store_codes(lo, hi):
+            cols = slice(CH * lo, CH * hi)
+            nc.sync.dma_start(
+                out=out_1[0].rearrange("p n t -> p (n t)").bitcast(I32)[:, cols], in_=o_codes[:, cols].bitcast(I32)
+            )
+
+        def quant_o(lo, hi, store):
             cols = slice(CH * lo, CH * hi)
             nc.vector.quantize_mx(
                 out=o_codes[:, cols].bitcast(FP8X4), scales=o_scales[:, cols], in_=o_bf[:, PACK * CH * lo : PACK * CH * hi]
             )
-            nc.sync.dma_start(
-                out=out_1[0].rearrange("p n t -> p (n t)").bitcast(I32)[:, cols], in_=o_codes[:, cols].bitcast(I32)
-            )
+            if store:
+                store_codes(lo, hi)
 
         for c in range(NCH):
             relu_h(c, c == 1)
@@ -303,9 +308,10 @@ def tile_picked_zshift_relu_po_kernel(
         for c in range(NCH):
             finish(c)
             cast_o(c)
-        quant_o(0, 2)
-        quant_o(2, 3)
-        quant_o(3, 4)
+        quant_o(0, 2, True)
+        quant_o(2, 3, False)
+        quant_o(3, 4, False)
+        store_codes(2, 4)
         for q in range(4):
             eng = nc.scalar if q % 2 else nc.sync
             eng.dma_start(

@@ -42,8 +42,7 @@ def tile_picked_zshift_relu_po_kernel(
         lists = [keep.tile([P, S // 16], U16, name="offs_sb"), keep.tile([P, S // 16], U16, name="prev_sb")]
         xs_win = sb("xs_win", [P, T], U8)
         ones = sb("ones", [P, P], F32)
-        xw_win = [placed("xw_win0", [P, 2 * T + N // 4], U32, 0)[:, :T], sb("xw_win1", [P, T], U32)[:, :]]
-        w5_raw = sb("w5_raw", [P, 2 * N], U8)[:, :]
+        xw_win = [placed("xw_win0", [P, 2 * T + N // 4], U32, 0)[:, :T], placed("xw_win1", [P, T], U32, 8 * T + N)[:, :]]
         gate_words = [sb(f"gate_words{a}", [P, PASSES * 2 * N], U8)[:, :] for a in range(2)]
         xs_g = [sb(f"xs_g{g}", [P, 2 * S], U8) for g in range(PASSES)]
         xw_g = [[sb(f"xw_g{a}{g}", [P, S], U32) for g in range(PASSES)] for a in range(2)]
@@ -103,7 +102,6 @@ def tile_picked_zshift_relu_po_kernel(
         load_gate_words(1)
         load_gate_scales(0)
         load_x_words(1)
-        nc.sync.dma_start(out=w5_raw.bitcast(I32), in_=w5_words[0].bitcast(I32))
         load_gate_scales(1)
         for a in range(2):
             nc.vector.tensor_copy(xs_g[0][:, S * a : S * (a + 1)], xs_win[:].indirect(lists[a][:]))
@@ -123,10 +121,8 @@ def tile_picked_zshift_relu_po_kernel(
         load_w(1, 1, 0, PACK, raw_late[:, PACK * H :])
         gather_words(0, 1)
         gather_words(1, 1)
-        nc.vector.tensor_copy(
-            out=w5_dealt[:].bitcast(U16).rearrange("p (t m) -> p t m", t=PACK),
-            in_=w5_raw.bitcast(U16).rearrange("p (m t) -> p t m", t=PACK),
-        )
+        w5_raw = placed("w5_raw", [P, 2 * N], U8, 8 * T + N)[:, :]
+        nc.sync.dma_start(out=w5_raw.bitcast(I32), in_=w5_words[0].bitcast(I32))
 
         r_ps = [psum.tile([P, N], F32, name=f"r_ps{c}", tag=f"rbank{c}") for c in range(NCH)]
 
@@ -223,12 +219,16 @@ def tile_picked_zshift_relu_po_kernel(
             h_pass(c, 0, 1)
         cast_w(1, 1, 0, PACK, 0, 320, True)
         cast_w(1, 1, 0, PACK, 320, H, False)
+        nc.scalar.copy(
+            out=w5_dealt[:].bitcast(U16).rearrange("p (t m) -> p t m", t=PACK),
+            in_=w5_raw.bitcast(U16).rearrange("p (m t) -> p t m", t=PACK),
+        )
         copy_gate(NCH - 1, w_raw[(1, 1, 0)][:, :, H - CH :])
         quantize_w(1, 1, 0, 256)
         quantize_w(1, 1, 256, H)
         for c in range(NCH):
             h_pass(c, 1, 1)
-        s5_dealt = sb("s5_dealt", [P, N], U8)
+        s5_dealt = sb("s5_dealt", [P, N], U8, "w_bf11")
         nc.vector.tensor_copy(
             out=s5_dealt[:].rearrange("p (t m) -> p t m", t=PACK), in_=s5_raw[:].rearrange("p (m t) -> p t m", t=PACK)
         )

@@ -145,9 +145,9 @@ def tile_picked_zshift_relu_po_kernel(
         w_codes = {(a, g): sb(f"w_codes{a}{g}", [P, H], U32) for a in range(2) for g in range(PASSES)}
         w_scales = {(a, g): sb(f"w_scales{a}{g}", [P, H], U8) for a in range(2) for g in range(PASSES)}
 
-        def cast_w(a, g, j0, j1, lo, hi, on_vector):
-            dst = w_bf[(a, g)][:].rearrange("p (t m j) -> p m j t", t=PACK, j=PACK)[:, lo // PACK : hi // PACK, j0:j1, :]
-            src = w_raw[(a, g, j0)][:, :, lo:hi].rearrange("p j (m t) -> p m j t", t=PACK)
+        def cast_w(a, g, u, lo, hi, on_vector):
+            dst = w_bf[(a, g)][:].rearrange("p (t m j) -> p m j t", t=PACK, j=PACK)[:, lo:hi, :, 2 * u : 2 * u + 2]
+            src = w_raw[(a, g, 0)].rearrange("p j (m t) -> p m j t", t=PACK)[:, lo:hi, :, 2 * u : 2 * u + 2]
             if on_vector:
                 nc.vector.tensor_copy(out=dst, in_=src)
             else:
@@ -196,8 +196,10 @@ def tile_picked_zshift_relu_po_kernel(
             r_pass(c, 0, 1)
         for c in range(NCH):
             r_pass(c, 1, 1)
-        cast_w(0, 0, 0, PACK, 0, H, True)
-        quantize_w(0, 0, 0, H)
+        cast_w(0, 0, 0, 0, P, True)
+        cast_w(0, 0, 1, 0, P, True)
+        quantize_w(0, 0, 0, 256)
+        quantize_w(0, 0, 256, H)
         for c in range(NCH):
             gate(c)
         for c in range(NCH // 2):
@@ -208,17 +210,22 @@ def tile_picked_zshift_relu_po_kernel(
             turn_gate(c)
         for c in range(NCH - 1):
             copy_gate(c, sb(f"sig{c}", [P, PACK, CH], F32)[:])
-        cast_w(1, 0, 0, PACK, 0, H, True)
-        quantize_w(1, 0, 0, H)
+        cast_w(1, 0, 0, 0, P, True)
+        cast_w(1, 0, 1, 0, P, True)
+        quantize_w(1, 0, 0, 256)
+        quantize_w(1, 0, 256, H)
         for c in range(NCH):
             h_pass(c, 1, 0)
-        cast_w(0, 1, 0, PACK, 0, 384, True)
-        cast_w(0, 1, 0, PACK, 384, H, False)
-        quantize_w(0, 1, 0, H)
+        cast_w(0, 1, 0, 0, P, True)
+        cast_w(0, 1, 1, 0, 64, True)
+        cast_w(0, 1, 1, 64, P, False)
+        quantize_w(0, 1, 0, 256)
+        quantize_w(0, 1, 256, H)
         for c in range(NCH):
             h_pass(c, 0, 1)
-        cast_w(1, 1, 0, PACK, 0, 320, True)
-        cast_w(1, 1, 0, PACK, 320, H, False)
+        cast_w(1, 1, 0, 0, P, True)
+        cast_w(1, 1, 1, 0, 32, True)
+        cast_w(1, 1, 1, 32, P, False)
         nc.scalar.copy(
             out=w5_dealt[:].bitcast(U16).rearrange("p (t m) -> p t m", t=PACK),
             in_=w5_raw.bitcast(U16).rearrange("p (m t) -> p t m", t=PACK),

@@ -118,9 +118,13 @@ def tile_picked_zshift_relu_po_kernel(
         load_w(0, 1, 0, PACK, raw_late[:, : PACK * H])
         for r in range(4):
             nc.sync.dma_start(out=s5_raw[r:P:32, :].bitcast(I32), in_=w5_scales[0].bitcast(I32)[r:16:4, :])
-        load_w(1, 1, 0, PACK, raw_late[:, PACK * H :])
-        gather_words(0, 1)
-        gather_words(1, 1)
+        last_rows = w4[512:, :].rearrange("(p j) c -> p j c", j=PACK)
+        last_raw = [raw_late[:, (PACK + 2 * i) * H : (PACK + 2 * i + 2) * H].rearrange("p (j c) -> p j c", j=PACK) for i in range(2)]
+        for i in range(2):
+            nc.sync.dma_start(out=last_raw[i], in_=last_rows[:, :, i * H // 2 : (i + 1) * H // 2])
+        for lo in (0, S // 2):
+            for a in range(2):
+                gather_words(a, 1, lo, lo + S // 2)
         w5_raw = placed("w5_raw", [P, 2 * N], U8, 8 * T + N)[:, :]
         nc.sync.dma_start(out=w5_raw.bitcast(I32), in_=w5_words[0].bitcast(I32))
 
@@ -148,6 +152,14 @@ def tile_picked_zshift_relu_po_kernel(
         def cast_w(a, g, u, lo, hi, on_vector):
             dst = w_bf[(a, g)][:].rearrange("p (t m j) -> p m j t", t=PACK, j=PACK)[:, lo:hi, :, 2 * u : 2 * u + 2]
             src = w_raw[(a, g, 0)].rearrange("p j (m t) -> p m j t", t=PACK)[:, lo:hi, :, 2 * u : 2 * u + 2]
+            if on_vector:
+                nc.vector.tensor_copy(out=dst, in_=src)
+            else:
+                nc.scalar.copy(out=dst, in_=src)
+
+        def cast_last(i, u, lo, hi, on_vector):
+            dst = w_bf[(1, 1)][:].rearrange("p (t m j) -> p m j t", t=PACK, j=PACK)[:, 64 * i + lo : 64 * i + hi, :, 2 * u : 2 * u + 2]
+            src = last_raw[i].rearrange("p j (m t) -> p m j t", t=PACK)[:, lo:hi, :, 2 * u : 2 * u + 2]
             if on_vector:
                 nc.vector.tensor_copy(out=dst, in_=src)
             else:
@@ -194,7 +206,6 @@ def tile_picked_zshift_relu_po_kernel(
 
         for c in range(NCH):
             r_pass(c, 0, 1)
-        for c in range(NCH):
             r_pass(c, 1, 1)
         cast_w(0, 0, 0, 0, P, True)
         cast_w(0, 0, 1, 0, P, True)
@@ -202,13 +213,11 @@ def tile_picked_zshift_relu_po_kernel(
         quantize_w(0, 0, 256, H)
         for c in range(NCH):
             gate(c)
-        for c in range(NCH // 2):
+        for c in range(NCH):
             turn_gate(c)
         for c in range(NCH):
             h_pass(c, 0, 0)
-        for c in range(NCH // 2, NCH):
-            turn_gate(c)
-        for c in range(NCH - 1):
+        for c in range(NCH):
             copy_gate(c, sb(f"sig{c}", [P, PACK, CH], F32)[:])
         cast_w(1, 0, 0, 0, P, True)
         cast_w(1, 0, 1, 0, P, True)
@@ -217,20 +226,20 @@ def tile_picked_zshift_relu_po_kernel(
         for c in range(NCH):
             h_pass(c, 1, 0)
         cast_w(0, 1, 0, 0, P, True)
-        cast_w(0, 1, 1, 0, 64, True)
-        cast_w(0, 1, 1, 64, P, False)
+        cast_w(0, 1, 1, 0, P, False)
         quantize_w(0, 1, 0, 256)
         quantize_w(0, 1, 256, H)
         for c in range(NCH):
             h_pass(c, 0, 1)
-        cast_w(1, 1, 0, 0, P, True)
-        cast_w(1, 1, 1, 0, 32, True)
-        cast_w(1, 1, 1, 32, P, False)
+        cast_last(0, 0, 0, 64, True)
+        cast_last(0, 1, 0, 64, False)
+        cast_last(1, 0, 0, 64, True)
+        cast_last(1, 1, 0, 24, True)
+        cast_last(1, 1, 24, 64, False)
         nc.scalar.copy(
             out=w5_dealt[:].bitcast(U16).rearrange("p (t m) -> p t m", t=PACK),
             in_=w5_raw.bitcast(U16).rearrange("p (m t) -> p t m", t=PACK),
         )
-        copy_gate(NCH - 1, w_raw[(1, 1, 0)][:, :, H - CH :])
         quantize_w(1, 1, 0, 256)
         quantize_w(1, 1, 256, H)
         for c in range(NCH):

@@ -99,9 +99,9 @@ def tile_picked_zshift_relu_po_kernel(
                 in_=x_scales.bitcast(I32)[:, r:16:4, :].rearrange("g q c -> q g c"),
             )
         load_x_words(0)
-        load_gate_words(1)
         load_gate_scales(0)
         load_x_words(1)
+        load_gate_words(1)
         load_gate_scales(1)
         for a in range(2):
             nc.vector.tensor_copy(xs_g[0][:, S * a : S * (a + 1)], xs_win[:].indirect(lists[a][:]))
@@ -226,22 +226,25 @@ def tile_picked_zshift_relu_po_kernel(
         for c in range(NCH):
             h_pass(c, 1, 0)
         cast_w(0, 1, 0, 0, P, True)
-        cast_w(0, 1, 1, 0, P, False)
+        cast_w(0, 1, 1, 0, 32, True)
+        cast_w(0, 1, 1, 32, P, False)
         quantize_w(0, 1, 0, 256)
         quantize_w(0, 1, 256, H)
         for c in range(NCH):
             h_pass(c, 0, 1)
         cast_last(0, 0, 0, 64, True)
         cast_last(0, 1, 0, 64, False)
+        for t in (2, 3, 0, 1):
+            quantize_w(1, 1, P * t, P * t + 64)
         cast_last(1, 0, 0, 64, True)
-        cast_last(1, 1, 0, 24, True)
-        cast_last(1, 1, 24, 64, False)
+        cast_last(1, 1, 0, 16, True)
+        cast_last(1, 1, 16, 64, False)
         nc.scalar.copy(
             out=w5_dealt[:].bitcast(U16).rearrange("p (t m) -> p t m", t=PACK),
             in_=w5_raw.bitcast(U16).rearrange("p (m t) -> p t m", t=PACK),
         )
-        quantize_w(1, 1, 0, 256)
-        quantize_w(1, 1, 256, H)
+        for t in range(PACK):
+            quantize_w(1, 1, P * t + 64, P * (t + 1))
         for c in range(NCH):
             h_pass(c, 1, 1)
         s5_dealt = sb("s5_dealt", [P, N], U8, "w_bf11")

@@ -41,21 +41,17 @@ def tile_picked_zshift_relu_po_kernel(
 
         lists = [keep.tile([P, S // 16], U16, name="offs_sb"), keep.tile([P, S // 16], U16, name="prev_sb")]
         xs_win = sb("xs_win", [P, T], U8)
-        ones = sb("ones", [P, P], F32)
+        warm_in = sb("warm_in", [P, 1], F32)
         xw_win = [placed("xw_win0", [P, 2 * T + N // 4], U32, 0)[:, :T], placed("xw_win1", [P, T], U32, 8 * T + N)[:, :]]
         gate_words = [sb(f"gate_words{a}", [P, PASSES * 2 * N], U8)[:, :] for a in range(2)]
         xs_g = [sb(f"xs_g{g}", [P, 2 * S], U8) for g in range(PASSES)]
         xw_g = [[sb(f"xw_g{a}{g}", [P, S], U32) for g in range(PASSES)] for a in range(2)]
         gate_scales = [sb(f"gate_scales{a}", [P, PASSES * N], U8) for a in range(2)]
         w5_dealt = sb("w5_dealt", [P, 2 * N], U8)
-        ident = sb("ident", [P, P], F32)
         warm_out = sb("warm_out", [P, 1], F32)
 
         nc.gpsimd.memset(xs_win[:].bitcast(I32), 0)
-        nc.gpsimd.memset(ones[:], 1.0)
-        nc.gpsimd.affine_select(
-            out=ident[:], in_=ones[:], compare_op=ALU.is_equal, fill=0.0, base=0, pattern=[[-1, P]], channel_multiplier=1
-        )
+        nc.vector.memset(warm_in[:], 0.0)
         for a in range(2):
             nc.vector.memset(gate_scales[a][:].bitcast(I32), 0)
         nc.vector.memset(xs_g[1][:].bitcast(I32), 0)
@@ -92,7 +88,7 @@ def tile_picked_zshift_relu_po_kernel(
         nc.sync.dma_start(lists[0][:], offs)
         nc.sync.dma_start(lists[1][:], prev)
         load_gate_words(0)
-        nc.scalar.activation(warm_out[:], ident[:, 0:1], ACT.Sigmoid)
+        nc.scalar.activation(warm_out[:], warm_in[:], ACT.Sigmoid)
         for r in range(4):
             nc.sync.dma_start(
                 out=xs_win[r:P:16, :].bitcast(I32),
@@ -128,22 +124,39 @@ def tile_picked_zshift_relu_po_kernel(
         w5_raw = placed("w5_raw", [P, 2 * N], U8, 8 * T + N)[:, :]
         nc.sync.dma_start(out=w5_raw.bitcast(I32), in_=w5_words[0].bitcast(I32))
 
-        r_ps = [psum.tile([P, N], F32, name=f"r_ps{c}", tag=f"rbank{c}") for c in range(NCH)]
-
-        def r_pass(c, a, g):
-            nc.tensor.matmul_mx(
-                out=r_ps[c][:],
-                lhsT=xw_g[a][g][:, CH * c : CH * (c + 1)].bitcast(FP8X4),
-                lhsT_scale=xs_g[g][:, S * a + CH * c : S * a + CH * (c + 1)],
-                rhs=gate_words[a][:, 2 * N * g : 2 * N * (g + 1)].bitcast(FP4X4),
-                rhs_scale=gate_scales[a][:, N * g : N * (g + 1)],
-                start=(a == 0 and g == 0),
-                stop=(a == 1 and g == 1),
-            )
-
+        dealt_words = [sb(f"dealt_words{a}", [P, PASSES * 2 * N], U8) for a in range(2)]
+        dealt_scales = {(a, g): sb(f"dealt_scales{a}{g}", [P, N], U8) for a in range(2) for g in range(PASSES)}
         for a in range(2):
-            for c in range(NCH):
-                r_pass(c, a, 0)
+            for g in range(PASSES):
+                cols = slice(2 * N * g, 2 * N * (g + 1))
+                nc.scalar.copy(
+                    out=dealt_words[a][:, cols].bitcast(U16).rearrange("p (t m) -> p t m", t=PACK),
+                    in_=gate_words[a][:, cols].bitcast(U16).rearrange("p (m t) -> p t m", t=PACK),
+                )
+                nc.gpsimd.tensor_copy(
+                    out=dealt_scales[(a, g)][:].rearrange("p (t m) -> p t m", t=PACK),
+                    in_=gate_scales[a][:, N * g : N * (g + 1)].rearrange("p (m t) -> p t m", t=PACK),
+                )
+
+        HALF = S // 2
+        r_ps = {
+            (i, u): psum.tile([P, 2, HALF], F32, name=f"r_ps{i}{u}", tag=f"rbank{2 * i + u}") for i in range(2) for u in range(2)
+        }
+
+        def r_pass(i, a, g):
+            for t in range(PACK):
+                nc.tensor.matmul_mx(
+                    out=r_ps[(i, t // 2)][:, t % 2, :],
+                    lhsT=dealt_words[a][:, 2 * N * g + 2 * P * t : 2 * N * g + 2 * P * (t + 1)].bitcast(FP4X4),
+                    lhsT_scale=dealt_scales[(a, g)][:, P * t : P * (t + 1)],
+                    rhs=xw_g[a][g][:, HALF * i : HALF * (i + 1)].bitcast(FP8X4),
+                    rhs_scale=xs_g[g][:, S * a + HALF * i : S * a + HALF * (i + 1)],
+                    start=(a == 0 and g == 0 and t % 2 == 0),
+                    stop=(a == 1 and g == 1 and t % 2 == 1),
+                )
+
+        for i in range(2):
+            r_pass(i, 0, 0)
 
         w_bf = {(a, g): sb(f"w_bf{a}{g}", [P, PACK * H], BF16) for a in range(2) for g in range(PASSES)}
         w_codes = {(a, g): sb(f"w_codes{a}{g}", [P, H], U32) for a in range(2) for g in range(PASSES)}
@@ -186,39 +199,20 @@ def tile_picked_zshift_relu_po_kernel(
                     stop=(a == 1 and g == 1 and t == PACK - 1),
                 )
 
-        sig = {}
-
-        def gate(c):
-            sig_t = sb(f"sig_rows{c}", [P, PACK, P], F32)[:]
-            nc.scalar.activation(sig_t, r_ps[c][:].rearrange("p (m t) -> p t m", t=PACK), ACT.Sigmoid)
-            sig[c] = sig_t
-
-        def turn_gate(c):
-            turned = psum.tile([P, PACK, CH], F32, name=f"turned{c}", tag=f"rbank{c}")
-            for t in range(PACK):
-                nc.tensor.transpose(turned[:, t, :], sig[c][:, t, :], ident[:])
-            sig[c] = turned
-
-        def copy_gate(c, dst):
-            turned = sig[c]
-            sig[c] = dst
-            nc.scalar.copy(sig[c], turned[:])
-
-        for c in range(NCH):
-            r_pass(c, 0, 1)
-            r_pass(c, 1, 1)
+        gate_half = [sb(f"gate_half{i}", [P, PACK, HALF], F32) for i in range(2)]
+        sig = {c: gate_half[c // 2][:, :, CH * (c % 2) : CH * (c % 2 + 1)] for c in range(NCH)}
+        for i in range(2):
+            r_pass(i, 0, 1)
+            r_pass(i, 1, 0)
+            r_pass(i, 1, 1)
+            for u in range(2):
+                nc.scalar.activation(gate_half[i][:, 2 * u : 2 * u + 2, :], r_ps[(i, u)][:], ACT.Sigmoid)
         cast_w(0, 0, 0, 0, P, True)
         cast_w(0, 0, 1, 0, P, True)
         quantize_w(0, 0, 0, 256)
         quantize_w(0, 0, 256, H)
         for c in range(NCH):
-            gate(c)
-        for c in range(NCH):
-            turn_gate(c)
-        for c in range(NCH):
             h_pass(c, 0, 0)
-        for c in range(NCH):
-            copy_gate(c, sb(f"sig{c}", [P, PACK, CH], F32)[:])
         cast_w(1, 0, 0, 0, P, True)
         cast_w(1, 0, 1, 0, P, True)
         quantize_w(1, 0, 0, 256)

@@ -199,14 +199,18 @@ def tile_picked_zshift_relu_po_kernel(
                     stop=(a == 1 and g == 1 and t == PACK - 1),
                 )
 
-        gate_half = [sb(f"gate_half{i}", [P, PACK, HALF], F32) for i in range(2)]
+        gate_half = [sb("gate_half0", [P, PACK, HALF], F32)[:], w_raw[(1, 0, 0)][:, :, HALF:]]
         sig = {c: gate_half[c // 2][:, :, CH * (c % 2) : CH * (c % 2 + 1)] for c in range(NCH)}
         for i in range(2):
             r_pass(i, 0, 1)
             r_pass(i, 1, 0)
             r_pass(i, 1, 1)
+
+        def gate(i):
             for u in range(2):
                 nc.scalar.activation(gate_half[i][:, 2 * u : 2 * u + 2, :], r_ps[(i, u)][:], ACT.Sigmoid)
+
+        gate(0)
         cast_w(0, 0, 0, 0, P, True)
         cast_w(0, 0, 1, 0, P, True)
         quantize_w(0, 0, 0, 256)
@@ -214,7 +218,9 @@ def tile_picked_zshift_relu_po_kernel(
         for c in range(NCH):
             h_pass(c, 0, 0)
         cast_w(1, 0, 0, 0, P, True)
-        cast_w(1, 0, 1, 0, P, True)
+        cast_w(1, 0, 1, 0, 64, True)
+        cast_w(1, 0, 1, 64, P, False)
+        gate(1)
         quantize_w(1, 0, 0, 256)
         quantize_w(1, 0, 256, H)
         for c in range(NCH):

@@ -34,10 +34,10 @@ def tile_picked_zshift_relu_po_kernel(
         late = ctx.enter_context(tc.tile_pool(name="late", bufs=1))
 
         def placed(name, shape, dtype, offset):
-            return late.tile(shape, dtype, name=name, align_bytes=64, offset=offset)
+            return late.tile(shape, dtype, name=name, align_bytes=256, offset=offset)
 
         def sb(name, shape, dtype, tag=None):
-            return keep.tile(shape, dtype, name=name, tag=tag or name, align_bytes=64)
+            return keep.tile(shape, dtype, name=name, tag=tag or name, align_bytes=256)
 
         lists = [keep.tile([P, S // 16], U16, name="offs_sb"), keep.tile([P, S // 16], U16, name="prev_sb")]
         xs_win = sb("xs_win", [P, T], U8)

@@ -21,6 +21,7 @@ PACK = 4
 PASSES = 2
 CH = 128
 NCH = S // CH
+S5_AT = 8 * T + 2 * N
 
 
 def tile_picked_zshift_relu_po_kernel(
@@ -33,8 +34,8 @@ def tile_picked_zshift_relu_po_kernel(
 
         late = ctx.enter_context(tc.tile_pool(name="late", bufs=1))
 
-        def placed(name, shape, dtype, offset):
-            return late.tile(shape, dtype, name=name, align_bytes=256, offset=offset)
+        def placed(name, shape, dtype, offset, align=256):
+            return late.tile(shape, dtype, name=name, align_bytes=align, offset=offset)
 
         def sb(name, shape, dtype, tag=None):
             return keep.tile(shape, dtype, name=name, tag=tag or name, align_bytes=256)
@@ -42,7 +43,7 @@ def tile_picked_zshift_relu_po_kernel(
         lists = [keep.tile([P, S // 16], U16, name="offs_sb"), keep.tile([P, S // 16], U16, name="prev_sb")]
         xs_win = sb("xs_win", [P, T], U8)
         warm_in = sb("warm_in", [P, 1], F32)
-        xw_win = [placed("xw_win0", [P, 2 * T + N // 4], U32, 0)[:, :T], placed("xw_win1", [P, T], U32, 8 * T + N)[:, :]]
+        xw_win = [placed("xw_win0", [P, 2 * T], U32, 0)[:, :T], placed("xw_win1", [P, T], U32, 8 * T)[:, :]]
         gate_words = [sb(f"gate_words{a}", [P, PASSES * 2 * N], U8)[:, :] for a in range(2)]
         xs_g = [sb(f"xs_g{g}", [P, 2 * S], U8) for g in range(PASSES)]
         xw_g = [[sb(f"xw_g{a}{g}", [P, S], U32) for g in range(PASSES)] for a in range(2)]
@@ -85,9 +86,9 @@ def tile_picked_zshift_relu_po_kernel(
         def gather_words(a, g, lo=0, hi=S):
             nc.vector.tensor_copy(xw_g[a][g][:, lo:hi], xw_win[g].indirect(lists[a][:, lo // 16 : hi // 16]))
 
+        load_gate_words(0)
         nc.sync.dma_start(lists[0][:], offs)
         nc.sync.dma_start(lists[1][:], prev)
-        load_gate_words(0)
         nc.scalar.activation(warm_out[:], warm_in[:], ACT.Sigmoid)
         for r in range(4):
             nc.sync.dma_start(
@@ -109,11 +110,7 @@ def tile_picked_zshift_relu_po_kernel(
         gather_words(0, 0, S // 2, S)
         gather_words(1, 0)
         raw_late = placed("raw_late", [P, 2 * PACK * H], F32, 0)
-        s5_raw = placed("s5_raw", [P, N], U8, 8 * T)
-        nc.vector.memset(s5_raw[:].bitcast(I32), 0)
         load_w(0, 1, 0, PACK, raw_late[:, : PACK * H])
-        for r in range(4):
-            nc.sync.dma_start(out=s5_raw[r:P:32, :].bitcast(I32), in_=w5_scales[0].bitcast(I32)[r:16:4, :])
         last_rows = w4[512:, :].rearrange("(p j) c -> p j c", j=PACK)
         last_raw = [raw_late[:, (PACK + 2 * i) * H : (PACK + 2 * i + 2) * H].rearrange("p (j c) -> p j c", j=PACK) for i in range(2)]
         for i in range(2):
@@ -121,8 +118,12 @@ def tile_picked_zshift_relu_po_kernel(
         for lo in (0, S // 2):
             for a in range(2):
                 gather_words(a, 1, lo, lo + S // 2)
-        w5_raw = placed("w5_raw", [P, 2 * N], U8, 8 * T + N)[:, :]
+        w5_raw = placed("w5_raw", [P, 2 * N], U8, 8 * T)[:, :]
+        s5_raw = placed("s5_raw", [P, N], U8, S5_AT)
+        nc.vector.memset(s5_raw[:].bitcast(I32), 0)
         nc.sync.dma_start(out=w5_raw.bitcast(I32), in_=w5_words[0].bitcast(I32))
+        for r in range(4):
+            nc.sync.dma_start(out=s5_raw[r:P:32, :].bitcast(I32), in_=w5_scales[0].bitcast(I32)[r:16:4, :])
 
         dealt_words = [sb(f"dealt_words{a}", [P, PASSES * 2 * N], U8) for a in range(2)]
         dealt_scales = {(a, g): sb(f"dealt_scales{a}{g}", [P, N], U8) for a in range(2) for g in range(PASSES)}
@@ -259,7 +260,10 @@ def tile_picked_zshift_relu_po_kernel(
         st = {}
 
         def relu_h(c, on_vector):
-            h_bf = sb(f"h_bf{c}", [P, CH * PACK], BF16)
+            if on_vector:
+                h_bf = placed(f"h_bf{c}", [P, CH * PACK], BF16, S5_AT + CH - 2 * CH * PACK, 64)
+            else:
+                h_bf = sb(f"h_bf{c}", [P, CH * PACK], BF16)
             dst = h_bf[:].rearrange("p (n t) -> p n t", t=PACK)
             src = h_ps[c][:].rearrange("p t n -> p n t")
             if on_vector:
@@ -270,7 +274,10 @@ def tile_picked_zshift_relu_po_kernel(
 
         def quant_h(c):
             h_codes = sb(f"h_codes{c}", [P, CH], U32)
-            h_scales = sb(f"h_scales{c}", [P, CH], U8)
+            if c == 1:
+                h_scales = sb(f"h_scales{c}", [P, CH], U8)
+            else:
+                h_scales = placed(f"h_scales{c}", [P, CH], U8, S5_AT + CH * max(c, 1), 64)
             nc.vector.quantize_mx(out=h_codes[:].bitcast(FP8X4), scales=h_scales[:], in_=st[("hbf", c)][:])
             st[("hq", c)] = (h_codes, h_scales)
 

@@ -21,7 +21,7 @@ PACK = 4
 PASSES = 2
 CH = 128
 NCH = S // CH
-S5_AT = 8 * T + 2 * N
+S5_AT = 8 * T + 4 * N
 
 
 def tile_picked_zshift_relu_po_kernel(
@@ -259,11 +259,15 @@ def tile_picked_zshift_relu_po_kernel(
         out_v = out_0.rearrange("(p t) n -> p t n", t=PACK)
         st = {}
 
+        h_bf_late = placed("h_bf_late", [P, 2 * CH * PACK], BF16, S5_AT + 2 * CH)
+
         def relu_h(c, on_vector):
-            if on_vector:
-                h_bf = placed(f"h_bf{c}", [P, CH * PACK], BF16, S5_AT + CH - 2 * CH * PACK, 64)
+            if c == 0:
+                h_bf = sb("h_bf0", [P, CH * PACK], BF16)
+            elif c == 1:
+                h_bf = placed("h_bf1", [P, CH * PACK], BF16, S5_AT + CH - 2 * CH * PACK, 64)
             else:
-                h_bf = sb(f"h_bf{c}", [P, CH * PACK], BF16)
+                h_bf = h_bf_late[:, CH * PACK * (c - 2) : CH * PACK * (c - 1)]
             dst = h_bf[:].rearrange("p (n t) -> p n t", t=PACK)
             src = h_ps[c][:].rearrange("p t n -> p n t")
             if on_vector:
@@ -274,10 +278,10 @@ def tile_picked_zshift_relu_po_kernel(
 
         def quant_h(c):
             h_codes = sb(f"h_codes{c}", [P, CH], U32)
-            if c == 1:
-                h_scales = sb(f"h_scales{c}", [P, CH], U8)
+            if c == 0:
+                h_scales = placed("h_scales0", [P, CH], U8, S5_AT + CH, 64)
             else:
-                h_scales = placed(f"h_scales{c}", [P, CH], U8, S5_AT + CH * max(c, 1), 64)
+                h_scales = sb(f"h_scales{c}", [P, CH], U8)
             nc.vector.quantize_mx(out=h_codes[:].bitcast(FP8X4), scales=h_scales[:], in_=st[("hbf", c)][:])
             st[("hq", c)] = (h_codes, h_scales)
 

@@ -21,6 +21,7 @@ PACK = 4
 PASSES = 2
 CH = 128
 NCH = S // CH
+HALF = S // 2
 S5_AT = 8 * T + 4 * N
 
 
@@ -98,14 +99,14 @@ def tile_picked_zshift_relu_po_kernel(
         load_x_words(0)
         load_gate_scales(0)
         load_x_words(1)
-        load_gate_words(1)
         load_gate_scales(1)
+        load_gate_words(1)
         for a in range(2):
             nc.vector.tensor_copy(xs_g[0][:, S * a : S * (a + 1)], xs_win[:].indirect(lists[a][:]))
         nc.sync.dma_start(out=xs_g[1][0:112, :].bitcast(I32), in_=xs_g[0][16:128, :].bitcast(I32))
-        raw_early = sb("raw_early", [P, 2 * PACK * H], F32, "xs_win")
+        raw_early = sb("raw_early", [P, 2 * PACK * H + PACK * HALF - P], F32, "xs_win")
         load_w(0, 0, 0, PACK, raw_early[:, : PACK * H])
-        load_w(1, 0, 0, PACK, raw_early[:, PACK * H :])
+        load_w(1, 0, 0, PACK, raw_early[:, PACK * H : 2 * PACK * H])
         gather_words(0, 0, 0, S // 2)
         gather_words(0, 0, S // 2, S)
         gather_words(1, 0)
@@ -139,7 +140,6 @@ def tile_picked_zshift_relu_po_kernel(
                     in_=gate_scales[a][:, N * g : N * (g + 1)].rearrange("p (m t) -> p t m", t=PACK),
                 )
 
-        HALF = S // 2
         r_ps = {
             (i, u): psum.tile([P, 2, HALF], F32, name=f"r_ps{i}{u}", tag=f"rbank{2 * i + u}") for i in range(2) for u in range(2)
         }
@@ -200,7 +200,7 @@ def tile_picked_zshift_relu_po_kernel(
                     stop=(a == 1 and g == 1 and t == PACK - 1),
                 )
 
-        gate_half = [sb("gate_half0", [P, PACK, HALF], F32)[:], w_raw[(1, 0, 0)][:, :, HALF:]]
+        gate_half = [sb("gate_half0", [P, PACK, HALF], F32)[:], raw_early[:, 2 * PACK * H - P :].rearrange("p (t n) -> p t n", t=PACK)]
         sig = {c: gate_half[c // 2][:, :, CH * (c % 2) : CH * (c % 2 + 1)] for c in range(NCH)}
         for i in range(2):
             r_pass(i, 0, 1)
@@ -218,9 +218,9 @@ def tile_picked_zshift_relu_po_kernel(
         quantize_w(0, 0, 256, H)
         for c in range(NCH):
             h_pass(c, 0, 0)
-        cast_w(1, 0, 0, 0, P, True)
-        cast_w(1, 0, 1, 0, 64, True)
-        cast_w(1, 0, 1, 64, P, False)
+        for u in range(2):
+            cast_w(1, 0, u, 0, 96, True)
+            cast_w(1, 0, u, 96, P, False)
         gate(1)
         quantize_w(1, 0, 0, 256)
         quantize_w(1, 0, 256, H)

@@ -189,7 +189,7 @@ def tile_picked_zshift_relu_po_kernel(
         h_ps = [psum.tile([P, PACK, CH], F32, name=f"h_ps{c}", tag=f"bank{c}") for c in range(NCH)]
 
         def h_pass(c, a, g):
-            for t in range(PACK):
+            for t in (2, 3, 0, 1) if (a, g) == (1, 1) else range(PACK):
                 nc.tensor.matmul_mx(
                     out=h_ps[c][:, t, :],
                     lhsT=w_codes[(a, g)][:, P * t : P * (t + 1)].bitcast(FP8X4),
@@ -197,7 +197,7 @@ def tile_picked_zshift_relu_po_kernel(
                     rhs=xw_g[a][g][:, CH * c : CH * (c + 1)].bitcast(FP8X4),
                     rhs_scale=xs_g[g][:, S * a + CH * c : S * a + CH * (c + 1)],
                     start=(a == 0 and g == 0 and t == 0),
-                    stop=(a == 1 and g == 1 and t == PACK - 1),
+                    stop=(a == 1 and g == 1 and t == 1),
                 )
 
         gate_half = [sb("gate_half0", [P, PACK, HALF], F32)[:], raw_early[:, 2 * PACK * H - P :].rearrange("p (t n) -> p t n", t=PACK)]
@@ -237,14 +237,14 @@ def tile_picked_zshift_relu_po_kernel(
         cast_last(0, 1, 0, 64, False)
         for t in (2, 3, 0, 1):
             quantize_w(1, 1, P * t, P * t + 64)
+        cast_last(1, 1, 0, 32, True)
+        cast_last(1, 1, 32, 64, False)
         cast_last(1, 0, 0, 64, True)
-        cast_last(1, 1, 0, 16, True)
-        cast_last(1, 1, 16, 64, False)
         nc.scalar.copy(
             out=w5_dealt[:].bitcast(U16).rearrange("p (t m) -> p t m", t=PACK),
             in_=w5_raw.bitcast(U16).rearrange("p (m t) -> p t m", t=PACK),
         )
-        for t in range(PACK):
+        for t in (2, 3, 0, 1):
             quantize_w(1, 1, P * t + 64, P * (t + 1))
         for c in range(NCH):
             h_pass(c, 1, 1)

@@ -233,8 +233,9 @@ def tile_picked_zshift_relu_po_kernel(
         quantize_w(0, 1, 256, H)
         for c in range(NCH):
             h_pass(c, 0, 1)
-        cast_last(0, 0, 0, 64, True)
         cast_last(0, 1, 0, 64, False)
+        cast_last(0, 0, 0, 48, True)
+        cast_last(0, 0, 48, 64, False)
         for t in (2, 3, 0, 1):
             quantize_w(1, 1, P * t, P * t + 64)
         cast_last(1, 1, 0, 32, True)

from contextlib import ExitStack

import concourse.mybir as mybir

K, T, S, H, N = 1024, 2048, 512, 512, 512
FLOPS = 2 * S * (2 * K * N + 2 * K * H + H * N)

F32 = mybir.dt.float32
BF16 = mybir.dt.bfloat16
I32 = mybir.dt.int32
U32 = mybir.dt.uint32
U16 = mybir.dt.uint16
U8 = mybir.dt.uint8
FP8X4 = mybir.dt.float8_e4m3fn_x4
FP4X4 = mybir.dt.float4_e2m1fn_x4
ACT = mybir.ActivationFunctionType
ALU = mybir.AluOpType

P = 128
PACK = 4
PASSES = 2
CH = 128
NCH = S // CH
HALF = S // 2
S5_AT = 8 * T + 4 * N


def tile_picked_zshift_relu_po_kernel(
    tc, x_words, x_scales, w1_words, w1_scales, w2_words, w2_scales, w3, w4, w5_words, w5_scales, offs, prev, out_0, out_1, out_2
):
    nc = tc.nc
    with ExitStack() as ctx:
        keep = ctx.enter_context(tc.tile_pool(name="keep", bufs=1))
        psum = ctx.enter_context(tc.psum_pool(name="psum", bufs=1))

        late = ctx.enter_context(tc.tile_pool(name="late", bufs=1))

        def placed(name, shape, dtype, offset, align=256):
            return late.tile(shape, dtype, name=name, align_bytes=align, offset=offset)

        def sb(name, shape, dtype, tag=None):
            return keep.tile(shape, dtype, name=name, tag=tag or name, align_bytes=256)

        lists = [keep.tile([P, S // 16], U16, name="offs_sb"), keep.tile([P, S // 16], U16, name="prev_sb")]
        xs_win = sb("xs_win", [P, T], U8)
        warm_in = sb("warm_in", [P, 1], F32)
        xw_win = [placed("xw_win0", [P, 2 * T], U32, 0)[:, :T], placed("xw_win1", [P, T], U32, 8 * T)[:, :]]
        gate_words = [sb(f"gate_words{a}", [P, PASSES * 2 * N], U8)[:, :] for a in range(2)]
        xs_g = [sb(f"xs_g{g}", [P, 2 * S], U8) for g in range(PASSES)]
        xw_g = [[sb(f"xw_g{a}{g}", [P, S], U32) for g in range(PASSES)] for a in range(2)]
        gate_scales = [sb(f"gate_scales{a}", [P, PASSES * N], U8) for a in range(2)]
        w5_dealt = sb("w5_dealt", [P, 2 * N], U8)
        warm_out = sb("warm_out", [P, 1], F32)

        nc.gpsimd.memset(xs_win[:].bitcast(I32), 0)
        nc.vector.memset(warm_in[:], 0.0)
        for a in range(2):
            nc.vector.memset(gate_scales[a][:].bitcast(I32), 0)
        nc.vector.memset(xs_g[1][:].bitcast(I32), 0)

        def load_gate_words(a):
            nc.sync.dma_start(
                out=gate_words[a].bitcast(I32).rearrange("p (g c) -> p g c", g=PASSES),
                in_=[w1_words, w2_words][a].bitcast(I32).rearrange("g p c -> p g c"),
            )

        def load_gate_scales(a):
            for r in range(4):
                nc.sync.dma_start(
                    out=gate_scales[a][r:P:32, :].bitcast(I32).rearrange("p (g c) -> p g c", g=PASSES),
                    in_=[w1_scales, w2_scales][a].bitcast(I32)[:, r:16:4, :].rearrange("g q c -> q g c"),
                )

        def load_x_words(g):
            nc.sync.dma_start(
                out=xw_win[g].bitcast(I32),
                in_=x_words[g].rearrange("p n t -> p (n t)").bitcast(I32),
            )

        w_raw = {}

        def load_w(a, g, j0, j1, dst):
            rows = [w3, w4][a][512 * g : 512 * (g + 1), :].rearrange("(p j) c -> p (j c)", j=PACK)
            nc.sync.dma_start(out=dst, in_=rows[:, H * j0 : H * j1])
            w_raw[(a, g, j0)] = dst.rearrange("p (j c) -> p j c", c=H)

        def gather_words(a, g, lo=0, hi=S):
            nc.vector.tensor_copy(xw_g[a][g][:, lo:hi], xw_win[g].indirect(lists[a][:, lo // 16 : hi // 16]))

        load_gate_words(0)
        nc.sync.dma_start(lists[0][:], offs)
        nc.sync.dma_start(lists[1][:], prev)
        nc.scalar.activation(warm_out[:], warm_in[:], ACT.Sigmoid)
        for r in range(4):
            nc.sync.dma_start(
                out=xs_win[r:P:16, :].bitcast(I32),
                in_=x_scales.bitcast(I32)[:, r:16:4, :].rearrange("g q c -> q g c"),
            )
        load_x_words(0)
        load_gate_scales(0)
        load_x_words(1)
        load_gate_scales(1)
        load_gate_words(1)
        for a in range(2):
            nc.vector.tensor_copy(xs_g[0][:, S * a : S * (a + 1)], xs_win[:].indirect(lists[a][:]))
        nc.sync.dma_start(out=xs_g[1][0:112, :].bitcast(I32), in_=xs_g[0][16:128, :].bitcast(I32))
        raw_early = sb("raw_early", [P, 2 * PACK * H + PACK * HALF - P], F32, "xs_win")
        load_w(0, 0, 0, PACK, raw_early[:, : PACK * H])
        load_w(1, 0, 0, PACK, raw_early[:, PACK * H : 2 * PACK * H])
        gather_words(0, 0, 0, S // 2)
        gather_words(0, 0, S // 2, S)
        gather_words(1, 0)
        raw_late = placed("raw_late", [P, 2 * PACK * H], F32, 0)
        load_w(0, 1, 0, PACK, raw_late[:, : PACK * H])
        last_rows = w4[512:, :].rearrange("(p j) c -> p j c", j=PACK)
        last_raw = [raw_late[:, (PACK + 2 * i) * H : (PACK + 2 * i + 2) * H].rearrange("p (j c) -> p j c", j=PACK) for i in range(2)]
        for i in range(2):
            nc.sync.dma_start(out=last_raw[i], in_=last_rows[:, :, i * H // 2 : (i + 1) * H // 2])
        for lo in (0, S // 2):
            for a in range(2):
                gather_words(a, 1, lo, lo + S // 2)
        w5_raw = placed("w5_raw", [P, 2 * N], U8, 8 * T)[:, :]
        s5_raw = placed("s5_raw", [P, N], U8, S5_AT)
        nc.vector.memset(s5_raw[:].bitcast(I32), 0)
        nc.sync.dma_start(out=w5_raw.bitcast(I32), in_=w5_words[0].bitcast(I32))
        for r in range(4):
            nc.sync.dma_start(out=s5_raw[r:P:32, :].bitcast(I32), in_=w5_scales[0].bitcast(I32)[r:16:4, :])

        dealt_words = [sb(f"dealt_words{a}", [P, PASSES * 2 * N], U8) for a in range(2)]
        dealt_scales = {(a, g): sb(f"dealt_scales{a}{g}", [P, N], U8) for a in range(2) for g in range(PASSES)}
        for a in range(2):
            for g in range(PASSES):
                cols = slice(2 * N * g, 2 * N * (g + 1))
                nc.scalar.copy(
                    out=dealt_words[a][:, cols].bitcast(U16).rearrange("p (t m) -> p t m", t=PACK),
                    in_=gate_words[a][:, cols].bitcast(U16).rearrange("p (m t) -> p t m", t=PACK),
                )
                nc.gpsimd.tensor_copy(
                    out=dealt_scales[(a, g)][:].rearrange("p (t m) -> p t m", t=PACK),
                    in_=gate_scales[a][:, N * g : N * (g + 1)].rearrange("p (m t) -> p t m", t=PACK),
                )

        r_ps = {
            (i, u): psum.tile([P, 2, HALF], F32, name=f"r_ps{i}{u}", tag=f"rbank{2 * i + u}") for i in range(2) for u in range(2)
        }

        def r_pass(i, a, g):
            for t in range(PACK):
                nc.tensor.matmul_mx(
                    out=r_ps[(i, t // 2)][:, t % 2, :],
                    lhsT=dealt_words[a][:, 2 * N * g + 2 * P * t : 2 * N * g + 2 * P * (t + 1)].bitcast(FP4X4),
                    lhsT_scale=dealt_scales[(a, g)][:, P * t : P * (t + 1)],
                    rhs=xw_g[a][g][:, HALF * i : HALF * (i + 1)].bitcast(FP8X4),
                    rhs_scale=xs_g[g][:, S * a + HALF * i : S * a + HALF * (i + 1)],
                    start=(a == 0 and g == 0 and t % 2 == 0),
                    stop=(a == 1 and g == 1 and t % 2 == 1),
                )

        for i in range(2):
            r_pass(i, 0, 0)

        w_bf = {(a, g): sb(f"w_bf{a}{g}", [P, PACK * H], BF16) for a in range(2) for g in range(PASSES)}
        w_codes = {(a, g): sb(f"w_codes{a}{g}", [P, H], U32) for a in range(2) for g in range(PASSES)}
        w_scales = {(a, g): sb(f"w_scales{a}{g}", [P, H], U8) for a in range(2) for g in range(PASSES)}

        def cast_w(a, g, u, lo, hi, on_vector):
            dst = w_bf[(a, g)][:].rearrange("p (t m j) -> p m j t", t=PACK, j=PACK)[:, lo:hi, :, 2 * u : 2 * u + 2]
            src = w_raw[(a, g, 0)].rearrange("p j (m t) -> p m j t", t=PACK)[:, lo:hi, :, 2 * u : 2 * u + 2]
            if on_vector:
                nc.vector.tensor_copy(out=dst, in_=src)
            else:
                nc.scalar.copy(out=dst, in_=src)

        def cast_last(i, u, lo, hi, on_vector):
            dst = w_bf[(1, 1)][:].rearrange("p (t m j) -> p m j t", t=PACK, j=PACK)[:, 64 * i + lo : 64 * i + hi, :, 2 * u : 2 * u + 2]
            src = last_raw[i].rearrange("p j (m t) -> p m j t", t=PACK)[:, lo:hi, :, 2 * u : 2 * u + 2]
            if on_vector:
                nc.vector.tensor_copy(out=dst, in_=src)
            else:
                nc.scalar.copy(out=dst, in_=src)

        def quantize_w(a, g, lo, hi):
            nc.vector.quantize_mx(
                out=w_codes[(a, g)][:, lo:hi].bitcast(FP8X4),
                scales=w_scales[(a, g)][:, lo:hi],
                in_=w_bf[(a, g)][:, PACK * lo : PACK * hi],
            )

        h_ps = [psum.tile([P, PACK, CH], F32, name=f"h_ps{c}", tag=f"bank{c}") for c in range(NCH)]

        def h_pass(c, a, g):
            for t in (2, 3, 0, 1) if (a, g) == (1, 1) else range(PACK):
                nc.tensor.matmul_mx(
                    out=h_ps[c][:, t, :],
                    lhsT=w_codes[(a, g)][:, P * t : P * (t + 1)].bitcast(FP8X4),
                    lhsT_scale=w_scales[(a, g)][:, P * t : P * (t + 1)],
                    rhs=xw_g[a][g][:, CH * c : CH * (c + 1)].bitcast(FP8X4),
                    rhs_scale=xs_g[g][:, S * a + CH * c : S * a + CH * (c + 1)],
                    start=(a == 0 and g == 0 and t == 0),
                    stop=(a == 1 and g == 1 and t == 1),
                )

        gate_half = [sb("gate_half0", [P, PACK, HALF], F32)[:], raw_early[:, 2 * PACK * H - P :].rearrange("p (t n) -> p t n", t=PACK)]
        sig = {c: gate_half[c // 2][:, :, CH * (c % 2) : CH * (c % 2 + 1)] for c in range(NCH)}
        for i in range(2):
            r_pass(i, 0, 1)
            r_pass(i, 1, 0)
            r_pass(i, 1, 1)

        def gate(i):
            for u in range(2):
                nc.scalar.activation(gate_half[i][:, 2 * u : 2 * u + 2, :], r_ps[(i, u)][:], ACT.Sigmoid)

        gate(0)
        cast_w(0, 0, 0, 0, P, True)
        cast_w(0, 0, 1, 0, P, True)
        quantize_w(0, 0, 0, 256)
        quantize_w(0, 0, 256, H)
        for c in range(NCH):
            h_pass(c, 0, 0)
        for u in range(2):
            cast_w(1, 0, u, 0, 96, True)
            cast_w(1, 0, u, 96, P, False)
        gate(1)
        quantize_w(1, 0, 0, 256)
        quantize_w(1, 0, 256, H)
        for c in range(NCH):
            h_pass(c, 1, 0)
        cast_w(0, 1, 0, 0, P, True)
        cast_w(0, 1, 1, 0, 32, True)
        cast_w(0, 1, 1, 32, P, False)
        quantize_w(0, 1, 0, 256)
        quantize_w(0, 1, 256, H)
        for c in range(NCH):
            h_pass(c, 0, 1)
        cast_last(0, 1, 0, 64, False)
        cast_last(0, 0, 0, 48, True)
        cast_last(0, 0, 48, 64, False)
        for t in (2, 3, 0, 1):
            quantize_w(1, 1, P * t, P * t + 64)
        cast_last(1, 1, 0, 32, True)
        cast_last(1, 1, 32, 64, False)
        cast_last(1, 0, 0, 64, True)
        nc.scalar.copy(
            out=w5_dealt[:].bitcast(U16).rearrange("p (t m) -> p t m", t=PACK),
            in_=w5_raw.bitcast(U16).rearrange("p (m t) -> p t m", t=PACK),
        )
        for t in (2, 3, 0, 1):
            quantize_w(1, 1, P * t + 64, P * (t + 1))
        for c in range(NCH):
            h_pass(c, 1, 1)
        s5_dealt = sb("s5_dealt", [P, N], U8, "w_bf11")
        nc.vector.tensor_copy(
            out=s5_dealt[:].rearrange("p (t m) -> p t m", t=PACK), in_=s5_raw[:].rearrange("p (m t) -> p t m", t=PACK)
        )


        o_codes = sb("o_codes", [P, S], U32)
        o_scales = sb("o_scales", [P, S], U8)
        out_v = out_0.rearrange("(p t) n -> p t n", t=PACK)
        st = {}

        h_bf_late = placed("h_bf_late", [P, 2 * CH * PACK], BF16, S5_AT + 2 * CH)

        def relu_h(c, on_vector):
            if c == 0:
                h_bf = sb("h_bf0", [P, CH * PACK], BF16)
            elif c == 1:
                h_bf = placed("h_bf1", [P, CH * PACK], BF16, S5_AT + CH - 2 * CH * PACK, 64)
            else:
                h_bf = h_bf_late[:, CH * PACK * (c - 2) : CH * PACK * (c - 1)]
            dst = h_bf[:].rearrange("p (n t) -> p n t", t=PACK)
            src = h_ps[c][:].rearrange("p t n -> p n t")
            if on_vector:
                nc.vector.tensor_scalar(dst, src, 0.0, None, ALU.max)
            else:
                nc.scalar.activation(dst, src, ACT.Relu)
            st[("hbf", c)] = h_bf

        def quant_h(c):
            h_codes = sb(f"h_codes{c}", [P, CH], U32)
            if c == 0:
                h_scales = placed("h_scales0", [P, CH], U8, S5_AT + CH, 64)
            else:
                h_scales = sb(f"h_scales{c}", [P, CH], U8)
            nc.vector.quantize_mx(out=h_codes[:].bitcast(FP8X4), scales=h_scales[:], in_=st[("hbf", c)][:])
            st[("hq", c)] = (h_codes, h_scales)

        def y_mm(c):
            h_codes, h_scales = st[("hq", c)]
            y_ps = psum.tile([P, PACK, CH], F32, name=f"y_ps{c}", tag=f"rbank{c}")
            for t in range(PACK):
                nc.tensor.matmul_mx(
                    out=y_ps[:, t, :],
                    lhsT=w5_dealt[:, 2 * P * t : 2 * P * (t + 1)].bitcast(FP4X4),
                    lhsT_scale=s5_dealt[:, P * t : P * (t + 1)],
                    rhs=h_codes[:].bitcast(FP8X4),
                    rhs_scale=h_scales[:],
                    start=True,
                    stop=True,
                )
            st[("y", c)] = y_ps

        def finish(c):
            cols = slice(CH * c, CH * (c + 1))
            o = sb(f"o{c}", [P, PACK, CH], F32)
            nc.vector.tensor_tensor(o[:], st[("y", c)][:], sig[c], ALU.mult)
            nc.sync.dma_start(out=out_v[:, :, cols], in_=o[:])
            st[("o", c)] = o

        o_bf = sb("o_bf", [P, S * PACK], BF16)

        def cast_o(c):
            nc.scalar.copy(
                out=o_bf[:, PACK * CH * c : PACK * CH * (c + 1)].rearrange("p (c i t) -> p c t i", i=4, t=PACK),
                in_=st[("o", c)][:].rearrange("p t (c i) -> p c t i", i=4),
            )

        def store_codes(lo, hi):
            cols = slice(CH * lo, CH * hi)
            nc.sync.dma_start(
                out=out_1[0].rearrange("p n t -> p (n t)").bitcast(I32)[:, cols], in_=o_codes[:, cols].bitcast(I32)
            )

        def quant_o(lo, hi, store):
            cols = slice(CH * lo, CH * hi)
            nc.vector.quantize_mx(
                out=o_codes[:, cols].bitcast(FP8X4), scales=o_scales[:, cols], in_=o_bf[:, PACK * CH * lo : PACK * CH * hi]
            )
            if store:
                store_codes(lo, hi)

        for c in range(NCH):
            relu_h(c, c == 1)
        for c in range(NCH):
            quant_h(c)
        for c in range(NCH):
            y_mm(c)
        for c in range(NCH):
            finish(c)
            cast_o(c)
        quant_o(0, 2, True)
        quant_o(2, 3, False)
        quant_o(3, 4, False)
        store_codes(2, 4)
        for q in range(4):
            eng = nc.scalar if q % 2 else nc.sync
            eng.dma_start(
                out=out_2[0].bitcast(I32)[4 * q : 4 * q + 4, :], in_=o_scales[32 * q : 32 * q + 4, :].bitcast(I32)
            )
